import numpy as np, ml_dtypes
CORES = [5,29,101,125,133,157,229,253]
N = 8
BF = ml_dtypes.bfloat16
S, R, NF, PH, LB, RO = 1024, 4096, 256, 512, 9, 4
def place(s, p):
    return ((s * p >> 4) + s + 37 * p) & (R - 1)
def records(rng):
    st = ((np.arange(8)[None, :] + rng.integers(0, 3, (N, 1))) % 3)[:, :, None, None]
    lo = np.where(st == 0, 0, np.where(st == 1, 64 * rng.integers(0, 4, (N, 8, 1, R)), 200 * (rng.random((N, 8, 1, R)) < 0.35))).astype(np.int32)
    span = np.where(st == 0, 256, np.where(st == 1, 64, 56)).astype(np.float32)
    x = np.minimum(lo + (rng.random((N, 8, 16, R), dtype=np.float32) * span).astype(np.int32), 255)
    u = rng.random((N, 8, 16, 1))
    th = np.where(st == 0, 1000 + 700 * u, np.where(st == 1, 256 + 2000 * u, 450 + 1150 * u)).astype(np.int64)
    return x, th
def parts(rng):
    var = rng.choice(np.array([0.2, 0.35, 0.5]), (N, 8, 1, 1)); emp = rng.choice(np.array([0.2, 0.45, 0.7]), (N, 8, 1, 1))
    tk = rng.integers(0, S, (N, 8, 16, S)) + S * (rng.random((N, 8, 16, S)) < var)
    fr = np.where(rng.random((N, 8, 16, NF)) < emp, -1, rng.integers(0, S * PH, (N, 8, 16, NF)))
    return tk, fr, rng.integers(0, S, (N, 8, NF)), rng.integers(0, NF, (N, 8, NF)), rng.integers(0, S, (N, 8, NF))
def pack(x, tk, fr, th, s, f, c):
    return {"x": np.ascontiguousarray(x.reshape(N, 128, R)).astype(np.float32).astype(BF), "sk": np.ascontiguousarray(tk.reshape(N, 128, S)).astype(np.int32),
            "fr": np.ascontiguousarray(fr.reshape(N, 128, NF)).astype(np.int32), "th": np.ascontiguousarray(th.reshape(N, 128, 1)).astype(np.int32),
            "gs": s.astype(np.int32), "gf": f.astype(np.int32), "gcl": c.astype(np.int32)}
def setup_inputs(rng):
    x, th = records(rng); tk, fr, s, f, c = parts(rng)
    return pack(x, tk, fr, th, s, f, c)
def setup_inputs_spread(rng):
    amp = np.exp2(8 * rng.random((N, 8, 1, R))).astype(np.float32)
    x = np.minimum((rng.random((N, 8, 16, R), dtype=np.float32) * amp).astype(np.int32), 255)
    x = np.where(rng.random((N, 8, 1, R)) < 0.0625, 255 - x, x)
    th = np.minimum(np.exp2(12 * rng.random((N, 8, 16, 1))).astype(np.int64), 4080)
    u = rng.random((N, 8, 16, S)); tk = np.minimum((2 * S * u * np.sqrt(u)).astype(np.int64), 2 * S - 1)
    v = rng.random((N, 8, 16, NF)); fr = np.where(rng.random(v.shape) < 0.3 * rng.random((N, 8, 1, 1)) + 0.1, -1, np.minimum((S * PH * v * v).astype(np.int64), S * PH - 1))
    w = rng.random((3, N, 8, NF)); w = w * w
    return pack(x, tk, fr, th, np.minimum((S * w[0]).astype(np.int64), S - 1), np.minimum((NF * w[1]).astype(np.int64), NF - 1), np.minimum((S * w[2]).astype(np.int64), S - 1))
def setup_inputs_ends(rng):
    one = rng.random((N, 8, 1, R)) < 0.5; each = rng.random((N, 8, 16, R)) < 0.5
    x = 255 * np.where(rng.random((N, 8, 1, R)) < 0.25, each, one).astype(np.int64)
    tk = (2 * S - 1) * rng.integers(0, 2, (N, 8, 16, S)); fr = np.where(rng.integers(0, 2, (N, 8, 16, NF)) == 1, S * PH - 1, -1)
    s = (S - 1) * rng.integers(0, 2, (N, 8, NF)); f = (NF - 1) * rng.integers(0, 2, (N, 8, NF)); c = (S - 1) * rng.integers(0, 2, (N, 8, NF))
    th = np.full((N, 8, 16, 1), 4080, np.int64)
    for a in range(N):
        for g in range(8):
            if g == 7: z = rng.permutation(15)[:9 if a % 2 == 0 else 7]
            else: z = rng.permutation(16)[:16 if g == 6 else 8]
            th[a, g, z, 0] = 0
    s[:, :, NF - 1] = S - 1; f[:, :, NF - 1] = NF - 1; c[:, :, NF - 1] = 0
    tk[::2, :, :, S - 1] = 2 * S - 1; tk[::2, :, :, 0] = 0; tk[:, 7, :, S - 1] = 2 * S - 1; tk[:, 7, :, 0] = 0
    x[..., place(S - 1, PH - 1)] = 255; x[..., place(S - 1, NF - 1)] = 255; x[..., place(0, NF - 1)] = 0
    return pack(x, tk, fr, th, s, f, c)
def setup_inputs_corners(rng):
    x, th = records(rng); tk, fr, s, f, c = parts(rng); i = np.arange(NF); even = i % 2 == 0
    near = np.array([[3, 21], [21, 3], [5, 19], [19, 5], [7, 9], [9, 7]])
    for a in range(N):
        o = rng.permutation(8)
        tk[a, o[0]] = tk[a, o[0]] & (S - 1); fr[a, o[0]] = -1
        tk[a, o[1]] = (tk[a, o[1]] & (S - 1)) + S; fr[a, o[1]] = -1
        tk[a, o[2]] = (tk[a, o[2]] & (S - 1)) + S
        fr[a, o[2]] = PH * rng.integers(0, S, (16, NF)) + np.where(rng.random((16, NF)) < 0.5, i, NF + i)
        f[a, o[3]] = i; fr[a, o[3]] = np.where(i % 2 == 0, -1, rng.integers(0, S * PH, (16, NF)))
        f[a, o[4]] = rng.choice(np.array([0, NF - 1]), NF); s[a, o[4]] = rng.choice(np.array([0, S - 1]), NF); c[a, o[4]] = np.where(rng.random(NF) < 0.5, s[a, o[4]], S - 1 - s[a, o[4]])
        fr[a, o[4]] = np.where(rng.random((16, NF)) < 0.4, -1, PH * rng.choice(np.array([0, S - 1]), (16, NF)) + rng.choice(np.array([0, NF - 1, NF, PH - 1]), (16, NF)))
        th[a, o[5]] = 4080; th[a, o[6]] = 0; th[a, o[7]] = 4080; th[a, o[7], rng.permutation(16)[:8]] = 0
        f[a, o[5]] = np.where(even, i, f[a, o[5]]); c[a, o[5]] = np.where(even, s[a, o[5]], c[a, o[5]]); fr[a, o[5]] = np.where(even, -1, fr[a, o[5]])
        pq = near[rng.integers(0, 6, NF)]
        s[a, o[6]] = np.where(even, S - pq[:, 0], s[a, o[6]]); c[a, o[6]] = np.where(even, S - pq[:, 1], c[a, o[6]])
    return pack(x, tk, fr, th, s, f, c)
def setup_inputs_ties(rng):
    v, th = records(rng); tk, fr, s, f, c = parts(rng)
    x = np.broadcast_to(60 * rng.integers(0, 5, (N, 8, 1, R)), (N, 8, 16, R)).copy()
    th = rng.choice(np.array([959, 960, 961, 1919, 1920, 1921]), (N, 8, 16, 1))
    off = rng.integers(0, 4, (N, 2, 16, R)) * (rng.random((N, 2, 1, R)) < 0.5)
    x[:, 1::4] = np.abs(255 * rng.integers(0, 2, (N, 2, 1, R)) - off)
    lev = np.array([0, 0, 0, 24, 24, 24, 4048, 4056, 4060, 4064, 4078, 4079, 4079, 4079, 4080, 4080])
    th[:, 1::4] = lev[np.argsort(rng.random((N, 2, 16, 1)), axis=2)]
    few = rng.integers(0, S, (N, 4, 3)); which = rng.integers(0, 3, (2, N, 4, NF))
    s[:, ::2] = np.take_along_axis(few, which[0], 2); c[:, ::2] = np.take_along_axis(few, which[1], 2); f[:, ::2] = rng.integers(0, 4, (N, 4, NF))
    return pack(x, tk, fr, th, s, f, c)
def check_inputs(d):
    bad = []
    for k, lo, hi in (("x", 0, 255), ("sk", 0, 2 * S - 1), ("fr", -1, S * PH - 1), ("th", 0, 4080), ("gs", 0, S - 1), ("gf", 0, NF - 1), ("gcl", 0, S - 1)):
        if k not in d: bad.append("no " + k); continue
        v = np.asarray(d[k]).astype(np.float64)
        if not (np.min(v) >= lo and np.max(v) <= hi): bad.append("range of " + k)
        elif np.any(v != np.floor(v)): bad.append("whole numbers in " + k)
    return bad
def reference(x, sk, fr, th, gs, gf, gcl):
    X = x.astype(np.float32).astype(np.int32).reshape(N, 8, 16, R); T = sk.astype(np.int64).reshape(N, 8, 16, S); lim = th.astype(np.int64).reshape(N, 8, 16, 1)
    own = fr.astype(np.int64).reshape(N, 8, 16, NF); F = np.concatenate([own, own], axis=3)
    i = np.arange(NF); mark = np.zeros((N, 8, 16, NF), bool); A = np.zeros((N, NF), np.int64)
    s = gs.astype(np.int64); f = gf.astype(np.int64); c = gcl.astype(np.int64); h = np.zeros_like(s) + i
    s0 = s; f0 = f; c0 = c
    def molecules(a, b):
        v = np.take_along_axis(T, a[:, :, None, :], 3); w = np.take_along_axis(F, b[:, :, None, :], 3)
        return np.where((v >= S) & (w >= 0), w, (v & (S - 1)) * PH + b[:, :, None, :]), (v >= S) & (w < 0)
    def pick(m):
        return np.take_along_axis(X, place(m >> LB, m & (PH - 1)).reshape(N, 8, 1, 16 * NF), 3)
    for rnd in range(RO):
        goal, _ = molecules(s, f); clause, hole = molecules(c, h)
        free = hole & (h == i)[:, :, None, :]; clause = np.where(free, goal, clause)
        D = np.add.reduce(np.abs(pick(goal) - pick(clause)), axis=2).astype(np.int64).reshape(N, 8, 16, NF)
        over = D > lim; clash = np.add.reduce(over.astype(np.int64), axis=2) >= 8 + (A & 1)[:, None, :]
        m = np.argmax(np.where(over, -1, D), axis=2)[:, :, None, :]
        gm = np.take_along_axis(goal, m, 2)[:, :, 0]; cm = np.take_along_axis(clause, m, 2)[:, :, 0]
        dm = np.take_along_axis(D, m, 2)[:, :, 0]; tm = np.take_along_axis(np.broadcast_to(lim, D.shape), m, 2)[:, :, 0]
        save = ~clash & (2 * dm < tm)
        bind = free & ~clash[:, :, None, :]
        own = np.where(mark & clash[:, :, None, :], -1, np.where(bind, goal, own))
        mark = (mark | bind) & ~(clash | save)[:, :, None, :]
        nxt = ((c0 * s0 >> 5) + c0 + 1) & (S - 1)
        s = np.where(clash, s0, gm >> LB); f = np.where(clash, f0, gm & (PH - 1))
        c = np.where(clash, nxt, cm >> LB); h = np.where(clash, i, cm & (PH - 1))
        s0 = np.where(save, s, s0); f0 = np.where(save, f, f0); c0 = np.where(clash, nxt, np.where(save, c, c0))
        A = np.add.reduce(clash.astype(np.int64), axis=1)
        F = np.concatenate([own, F[..., NF:]], axis=3)
        if rnd < RO - 1:
            d = 1 + rnd % (N - 1); col = np.take_along_axis(F, f[:, :, None, :], 3)
            F = np.concatenate([own, np.roll(col, d, axis=0)], axis=3); s = np.roll(s, d, axis=0); f = np.zeros_like(s) + NF + i
    return {"yf": np.where(own < 0, -1, 2 * own + mark).reshape(N, 128, NF).astype(np.float32), "yg": (PH * s + f).astype(np.float32), "yc": (PH * c + h).astype(np.float32),
            "ysg": (PH * s0 + f0).astype(np.float32), "yk": c0.astype(np.float32)}

@@ -1,0 +1,473 @@
+from concourse.bass import DstId, RemoteDMATransfer
+from concourse.mybir import AluOpType as OP, ActivationFunctionType as AF
+
+N = 8
+RO = 4
+NEG = -8388608.0
+B = 1 << 21
+KE = 592 * 1024 + 16
+PARTS = [(0, 4), (4, 8), (8, 12), (12, 14), (14, 16)]
+SUMS = [(0, 8, "ab0 ab1"), (8, 12, "ab2"), (12, 16, "ab3 ab4")]
+LOADS = ["l_gs0", "l_gs1", "l_gf0", "l_gf1", "l_gc0", "l_gc1", "l_gfr", "l_fr", "l_sk", "l_th", "l_x0", "l_x1"]
+
+SCRATCH = {
+    "XR": ("sbuf", [128, 4096], "bfloat16"),
+    "SKI": ("sbuf", [128, 1024], "int32"), "SKU": ("sbuf", [128, 1024], "float32"), "SKV": ("sbuf", [128, 1024], "float32"),
+    "FRI": ("sbuf", [128, 256], "int32"), "FRQ": ("sbuf", [128, 256], "int32"), "OW": ("sbuf", [128, 256], "float32"),
+    "BASE": ("sbuf", [128, 256], "float32"), "MK": ("sbuf", [128, 256], "float32"), "YA": ("sbuf", [128, 256], "float32"),
+    "FLG": ("sbuf", [128, 256], "float32"),
+    "F0": ("sbuf", [128, 528], "float32"), "F1": ("sbuf", [128, 528], "float32"),
+    "F2": ("sbuf", [128, 528], "float32"), "F3": ("sbuf", [128, 528], "float32"),
+    "COL0": ("sbuf", [128, 272], "float32"), "COL1": ("sbuf", [128, 272], "float32"), "COL2": ("sbuf", [128, 272], "float32"),
+    "RB0": ("sbuf", [128, 68], "float32"), "RB2": ("sbuf", [128, 68], "float32"),
+    "TT": ("sbuf", [128, 96], "int32"), "TX": ("sbuf", [128, 96], "int32"), "TA": ("sbuf", [128, 48], "float32"),
+    "TB": ("sbuf", [128, 48], "float32"), "TL": ("sbuf", [128, 48], "float32"),
+    "GFR": ("sbuf", [8, 256], "int32"), "GFB": ("sbuf", [8, 256], "bfloat16"),
+    "THI": ("sbuf", [128, 1], "int32"), "THF": ("sbuf", [128, 1], "float32"), "THD": ("sbuf", [128, 256], "float32"),
+    "THA": ("sbuf", [128, 256], "float32"), "THB": ("sbuf", [128, 256], "float32"), "THW": ("sbuf", [128, 256], "int32"),
+    "ONEB": ("sbuf", [128, 256], "bfloat16"), "ONEF": ("sbuf", [128, 128], "float32"),
+    "R16": ("sbuf", [16, 256], "bfloat16"), "R8": ("sbuf", [8, 128], "bfloat16"),
+    "IDF": ("sbuf", [128, 128], "float32"), "IDB": ("sbuf", [128, 128], "bfloat16"),
+    "BLKB": ("sbuf", [128, 128], "bfloat16"), "NBLK": ("sbuf", [128, 128], "bfloat16"), "BLKF": ("sbuf", [128, 128], "float32"),
+    "DIAG": ("sbuf", [128, 256], "bfloat16"), "SQ": ("sbuf", [128, 2048], "bfloat16"), "SWP": ("sbuf", [128, 512], "float32"),
+    "KB": ("sbuf", [128, 256], "bfloat16"), "RST": ("sbuf", [128, 512], "bfloat16"),
+    "IOT": ("sbuf", [128, 256], "float32"), "BIA": ("sbuf", [128, 256], "float32"), "BG": ("sbuf", [128, 256], "float32"),
+    "BH": ("sbuf", [128, 256], "float32"),
+    "C16": ("sbuf", [128, 16], "float32"), "PIO": ("sbuf", [128, 16], "int32"), "PM": ("sbuf", [128, 16], "int32"),
+    "LIK": ("sbuf", [128, 16], "float32"), "MUI": ("sbuf", [128, 16], "int32"), "MU1": ("sbuf", [128, 16], "float32"), "MU0": ("sbuf", [128, 16], "float32"),
+    "BC15": ("sbuf", [128, 16], "uint16"), "BCC": ("sbuf", [128, 16], "uint16"),
+    "SL": ("sbuf", [128, 16], "uint16"), "FL": ("sbuf", [128, 16], "uint16"), "CL": ("sbuf", [128, 16], "uint16"), "HL": ("sbuf", [128, 16], "uint16"),
+    "CG": ("sbuf", [128, 256], "float32"), "CC": ("sbuf", [128, 256], "float32"), "XC": ("sbuf", [128, 256], "float32"), "MG": ("sbuf", [128, 256], "int32"),
+    "XI": ("sbuf", [128, 512], "int32"), "PI": ("sbuf", [128, 256], "int32"), "QI": ("sbuf", [128, 256], "int32"),
+    "ZI": ("sbuf", [128, 256], "int32"), "RI": ("sbuf", [128, 256], "int32"), "RL": ("sbuf", [128, 512], "uint16"),
+    "U": ("sbuf", [128, 4096], "bfloat16"), "DB": ("sbuf", [128, 4096], "bfloat16"),
+    "AB": ("sbuf", [128, 16, 16, 16], "bfloat16"),
+    "XF": ("sbuf", [128, 512], "float32"), "XT": ("sbuf", [128, 16, 2, 16], "float32"),
+    "NOV": ("sbuf", [128, 256], "bfloat16"), "NS": ("sbuf", [128, 256], "bfloat16"), "SV": ("sbuf", [128, 256], "bfloat16"),
+    "SB": ("sbuf", [128, 16], "bfloat16"), "KY": ("sbuf", [128, 256], "float32"), "KM": ("sbuf", [128, 256], "float32"), "MASK": ("sbuf", [128, 256], "bfloat16"),
+    "MX": ("sbuf", [128, 512], "float32"), "SC": ("sbuf", [128, 512], "float32"),
+    "EX": ("sbuf", [128, 256], "bfloat16"), "EV": ("sbuf", [128, 256], "bfloat16"), "EH": ("sbuf", [128, 256], "float32"),
+    "LF": ("sbuf", [128, 512], "float32"), "LI": ("sbuf", [128, 256], "int32"),
+    "FLD": ("sbuf", [128, 128], "float32"), "FLT": ("sbuf", [128, 128], "float32"), "FO": ("sbuf", [128, 64], "float32"), "FP": ("sbuf", [128, 64], "float32"),
+    "YO": ("sbuf", [128, 256], "float32"), "YM": ("sbuf", [128, 256], "float32"),
+    "P0": ("psum", [128, 2, 16, 16], "float32"), "P1": ("psum", [128, 2, 8, 2, 16], "float32"), "P2": ("psum", [128, 512], "float32"),
+    "P3": ("psum", [128, 512], "float32"), "P4": ("psum", [128, 512], "float32"), "P5": ("psum", [128, 512], "float32"),
+    "P6": ("psum", [128, 512], "float32"), "P7": ("psum", [128, 2, 8, 2, 16], "float32"),
+}
+SEMAPHORES = LOADS + ["v", "s", "pe", "gc", "out", "sent", "in0", "in2", "arr0", "arr1", "arr2"]
+
+
+def routes(topo, a, b):
+    if topo.may_write(a, b):
+        return []
+    return [c for c in topo.cores_of(a) if c != a and topo.may_write(c, b)]
+
+
+def only(m, n):
+    return sum(1 << e for e in m[:n])
+
+
+def relay(g, core, T, topo):
+    sent = 0
+    for t in range(RO - 1):
+        d = 1 + t % (N - 1)
+        for r in range(N):
+            a, b = T.cores[r], T.cores[(r + d) % N]
+            if a not in topo.cores_of(core):
+                continue
+            rel = routes(topo, a, b)
+            if core not in rel:
+                continue
+            k, w = rel.index(core), 272 // len(rel)
+            g.wait_ge(T.sem["in%d" % t], 4)
+            rid, pid = topo.addr(b, core)
+            g.remote_dma(T["F%d" % (t + 1)][:, 256 + k * w:256 + (k + 1) * w], T["RB%d" % t][:, 0:w], T.sem["arr%d" % t], T.sem.sent,
+                         pid, rid, topo.mask(core, b))
+            sent += len(topo.engines(core, b))
+    if sent:
+        g.wait_ge(T.sem.sent, sent)
+
+
+def rank_program(g, core, T, topo):
+    rank = T.rank_of(core)
+    if rank is None:
+        return relay(g, core, T, topo)
+    ENG = {"v": g.vector, "s": g.scalar, "pe": g.tensor, "gc": g, "sync": g.sync}
+    cnt, seen, wr, rd = {}, {}, {}, {}
+
+    def before(q, reads, writes):
+        need = {}
+        for k in reads:
+            for tok in wr.get(k, []):
+                need[tok[1]] = max(need.get(tok[1], 0), tok[2])
+        for k in writes:
+            for tok in wr.get(k, []) + rd.get(k, []):
+                if tok[0] != q or q != "pe":
+                    need[tok[1]] = max(need.get(tok[1], 0), tok[2])
+        for s in sorted(need):
+            if seen.get((q, s), 0) < need[s]:
+                ENG[q].wait_ge(T.sem[s], need[s])
+                seen[(q, s)] = need[s]
+
+    def after(q, ins, sem, n, reads, writes):
+        cnt[sem] = cnt.get(sem, 0) + n
+        ins.then_inc(T.sem[sem], n)
+        tok = (q, sem, cnt[sem])
+        for k in writes:
+            wr[k] = [tok]
+            rd[k] = []
+        for k in reads:
+            rd.setdefault(k, []).append(tok)
+
+    def run(q, fn, reads, writes, *a, **kw):
+        reads, writes = reads.split(), writes.split()
+        before(q, reads, writes)
+        after(q, fn(*a, **kw), q, 1, reads, writes)
+
+    def load(q, out, in_, sem, key, reads=""):
+        reads = reads.split()
+        before(q, reads, [key])
+        after("dma_" + sem, ENG[q].dma_start(out, in_), sem, 16, reads, [key])
+
+    def arrive(sem, n, keys):
+        for k in keys.split():
+            wr[k] = [("net", sem, n)]
+            rd[k] = []
+
+    V = g.vector
+
+    def tt(reads, w, out, a, b, op):
+        run("v", V.tensor_tensor, reads, w, out, a, b, op)
+
+    def ts(reads, w, out, a, s1, op0, s2=None, op1=None):
+        if op1 is None:
+            run("v", V.tensor_scalar, reads, w, out, a, s1, None, op0)
+        else:
+            run("v", V.tensor_scalar, reads, w, out, a, s1, s2, op0, op1)
+
+    def cp(reads, w, out, a):
+        run("v", V.tensor_copy, reads, w, out, a)
+
+    def act(reads, w, out, a, func=AF.Copy, scale=1.0):
+        if scale == 1.0:
+            run("s", g.scalar.activation, reads, w, out, a, func)
+        else:
+            run("s", g.scalar.activation, reads, w, out, a, func, scale=scale)
+
+    def mms(reads, w, calls):
+        reads, w = reads.split(), w.split()
+        before("pe", reads, w)
+        for c in calls:
+            ins = g.tensor.matmul(*c)
+        after("pe", ins, "pe", 1, reads, w)
+
+    def lf(j):
+        return T.LF[:, 16 * j:16 * j + 16]
+
+    def li(j):
+        return T.LI[:, 16 * j:16 * j + 16]
+
+    load("sync", T.TT[:, 0:16], T.gs[:], "l_gs0", "tt0")
+    load("sync", T.TT[:, 16:32], T.gs[:], "l_gs1", "tt1")
+    load("sync", T.GFR[:], T.gf[:], "l_gfr", "gfr")
+    load("sync", T.SKI[:], T.sk[:], "l_sk", "ski")
+    load("sync", T.XR[:, 592:4096], T.x[:, 0:3504], "l_x0", "xr0")
+    load("s", T.TT[:, 32:48], T.gf[:], "l_gf0", "tt2")
+    load("s", T.TT[:, 48:64], T.gf[:], "l_gf1", "tt3")
+    load("s", T.FRI[:], T.fr[:], "l_fr", "fri")
+    load("s", T.TT[:, 64:80], T.gcl[:], "l_gc0", "tt4")
+    load("s", T.TT[:, 80:96], T.gcl[:], "l_gc1", "tt5")
+    load("s", T.XR[:, 0:592], T.x[:, 3504:4096], "l_x1", "xr1")
+    load("s", T.THI[:], T.th[:], "l_th", "thi")
+    XRK = "xr0 xr1 "
+
+    run("v", V.memset, "", "oneb", T.ONEB[:], 1.0)
+    run("v", V.memset, "", "onef", T.ONEF[:], 1.0)
+    sel = lambda o, i, p, r, w: run("gc", g.affine_select, r, w, o, i, p, OP.is_equal, 0.0, 0, 1)
+    iota = lambda o, p, base, cm, w: run("gc", g.iota, "", w, o, p, base, cm, allow_small_or_imprecise_dtypes=True)
+    iota(T.C16[:], [[16, 16]], KE, 0, "c16")
+    iota(T.PIO[:], [[0, 16]], 0, 1, "pio")
+    sel(T.R8[:], T.ONEB[0:8, 0:128], [[-1, 8], [0, 16]], "oneb", "r8")
+    sel(T.R16[:], T.ONEB[0:16, :], [[0, 16], [-1, 16]], "oneb", "r16")
+    iota(T.IOT[:], [[1, 256]], 0, 0, "iot")
+    sel(T.IDF[:], T.ONEF[:], [[-1, 128]], "onef", "idf")
+    iota(T.KB[:], [[0, 16], [-1, 16]], 15, 0, "kb")
+    iota(T.BIA[:], [[1, 256]], 256, 0, "bia")
+    for j in range(8):
+        act("iot", "sq", T.SQ[:, 256 * j:256 * j + 256], T.IOT[:], AF.Copy, 0.0)
+    for j in range(2):
+        act("iot", "swp", T.SWP[:, 256 * j:256 * j + 256], T.IOT[:], AF.Copy, 0.0)
+    ts("pio", "pm", T.PM[:], T.PIO[:], 15, OP.bitwise_and)
+    ts("pio", "mui", T.MUI[:], T.PIO[:], 4, OP.arith_shift_right, 1, OP.bitwise_and)
+    cp("mui", "mu1", T.MU1[:], T.MUI[:])
+    ts("mui", "mu0", T.MU0[:], T.MUI[:], -1.0, OP.mult, 1.0, OP.add)
+    tt("pm c16", "lik", T.LIK[:], T.PM[:], T.C16[:], OP.add)
+    ts("c16", "bc15", T.BC15[:], T.C16[:], float(15 - KE), OP.add)
+    ts("c16", "bcc", T.BCC[:], T.C16[:], float(-KE), OP.add, 0.0625, OP.mult)
+    mms("r8", "p4", [(T.P4[:, 0:128], T.R8[:], T.R8[:], True, True)])
+    mms("r16", "p3", [(T.P3[:, 0:256], T.R16[:, 0:128], T.R16[:], True, True)])
+
+    run("v", V.transpose, "tt0 tt1 tt2 tt3 tt4 tt5", "tx", T.TX[:], T.TT[:])
+    for j in range(3):
+        ts("tx mu0", "ta%d" % j, T.TA[:, 16 * j:16 * j + 16], T.TX[:, 32 * j:32 * j + 16], T.MU0[:, 0:1], OP.mult)
+        ts("tx mu1", "tb%d" % j, T.TB[:, 16 * j:16 * j + 16], T.TX[:, 32 * j + 16:32 * j + 32], T.MU1[:, 0:1], OP.mult)
+    tt("ta0 ta1 ta2 tb0 tb1 tb2", "tl", T.TL[:], T.TA[:], T.TB[:], OP.add)
+    cp("tl", "sl", T.SL[:], T.TL[:, 0:16])
+    cp("tl", "fl", T.FL[:], T.TL[:, 16:32])
+    cp("tl", "cl", T.CL[:], T.TL[:, 32:48])
+    ts("tl", "l2", lf(2), T.TL[:, 0:16], 1024.0, OP.mult, float(KE), OP.add)
+    tt("tl l2", "l0", lf(0), T.TL[:, 16:32], lf(2), OP.add)
+    cp("tl", "l1", lf(1), T.TL[:, 32:48])
+    cp("gfr", "gfb", T.GFB[:], T.GFR[:])
+    mms("r8 gfb", "p2", [(T.P2[:, 0:256], T.R8[:], T.GFB[:], True, True)])
+    act("p2", "bg", T.BG[:], T.P2[:, 0:256])
+    ts("fri", "frq", T.FRQ[:], T.FRI[:], 511, OP.bitwise_and)
+    ts("fri", "p6", T.P6[:, 0:256], T.FRI[:], 2.0, OP.mult, float(KE), OP.add)
+    ts("fri", "p5", T.P5[:, 0:256], T.FRI[:], 0.0, OP.is_lt, NEG, OP.mult)
+    tt("p6 frq", "ow", T.OW[:], T.P6[:, 0:256], T.FRQ[:], OP.subtract)
+    tt("p5 ow", "f0o", T.F0[:, 0:256], T.P5[:, 0:256], T.OW[:], OP.add)
+    act("f0o", "f0g", T.F0[:, 256:512], T.F0[:, 0:256])
+    act("f0o", "base", T.BASE[:], T.F0[:, 0:256])
+    ts("ski", "sku", T.SKU[:], T.SKI[:], 1024.0, OP.mult, float(KE + B), OP.add)
+    for j, p in ((0, "P5"), (1, "P6")):
+        cs = slice(512 * j, 512 * j + 512)
+        ts("ski", p.lower(), T[p][:], T.SKI[:, cs], 1024.0, OP.is_ge, float(-(1 << 20) - 2 * B), OP.mult)
+        tt(p.lower() + " sku", "skv", T.SKV[:, cs], T[p][:], T.SKU[:, cs], OP.add)
+    wr["skv"] = [("v", "v", cnt["v"])]
+
+    def late_constants():
+        act("p4", "blkb", T.BLKB[:], T.P4[:, 0:128])
+        act("p3", "diag", T.DIAG[:], T.P3[:, 0:256])
+        act("p4", "blkf", T.BLKF[:], T.P4[:, 0:128])
+        act("p4", "nblk", T.NBLK[:], T.P4[:, 0:128], AF.Copy, -1.0)
+        for q in range(16):
+            act("p4", "sq", T.SQ[:, 128 * q + q:128 * q + 128:16], T.P4[:, q:128:16], AF.Copy, 16.0)
+        for u in range(2):
+            for gl in range(2):
+                for a in range(4):
+                    o = 128 * (2 * u + gl) + 32 * a + 16 * gl
+                    act("idf", "swp", T.SWP[:, o:o + 16], T.IDF[:, 32 * a + 16 * u:32 * a + 16 * u + 16])
+        act("idf", "idb", T.IDB[:], T.IDF[:], AF.Copy, -NEG)
+    late_constants()
+
+    def th_tables():
+        cp("thi", "thf", T.THF[:], T.THI[:])
+        ts("diag thf", "thd", T.THD[:], T.DIAG[:], T.THF[:, 0:1], OP.mult)
+        mms("blkf thd", "p2", [(T.P2[:, 0:256], T.BLKF[:], T.THD[:], True, True)])
+        ts("p2", "thw", T.THW[:], T.P2[:, 0:256], -1.0, OP.add)
+        ts("p2", "tha", T.THA[:], T.P2[:, 0:256], 16.0, OP.mult, 15.0, OP.add)
+        ts("thw", "thx", T.THW[:], T.THW[:], 1, OP.arith_shift_right)
+        ts("thx", "thb", T.THB[:], T.THW[:], 16.0, OP.mult, 15.0, OP.add)
+        ts("kb", "rst0", T.RST[:, 0:256], T.KB[:], 15.0, OP.is_lt)
+        ts("kb", "rst1", T.RST[:, 256:512], T.KB[:], 15.0, OP.is_lt)
+        run("v", V.memset, "", "thr", lf(3), 8.0)
+        run("v", V.memset, "", "mk", T.MK[:], NEG)
+
+    def new_saved_clause():
+        cp("l0", "i0", li(0), lf(0))
+        ts("i0", "i1", li(1), li(0), 10, OP.arith_shift_right, 2047, OP.bitwise_and)
+        ts("i1", "l5", lf(5), li(1), -592.0, OP.add)
+        tt("l5 l1", "i2", li(2), lf(5), lf(1), OP.mult)
+        ts("i2", "i3", li(3), li(2), 5, OP.arith_shift_right)
+        ts("l1", "l6", lf(6), lf(1), 1.0, OP.add)
+        tt("i3 l6", "i4", li(4), li(3), lf(6), OP.add)
+        ts("i4", "i5", li(5), li(4), 1023, OP.bitwise_and)
+        ts("i5", "l7", lf(7), li(5), 1024.0, OP.mult)
+        tt("l7 lik", "l4", lf(4), lf(7), T.LIK[:], OP.add)
+
+    def recs(o, key):
+        X = T.XI[:, o:o + 256]
+        ts("xi" + key, "pi", T.PI[:], X, 10, OP.arith_shift_right, 2047, OP.bitwise_and)
+        ts("xi" + key, "qi", T.QI[:], X, 1023, OP.bitwise_and)
+        tt("pi qi", "zi", T.ZI[:], T.PI[:], T.QI[:], OP.mult)
+        ts("zi", "ri", T.RI[:], T.ZI[:], 4, OP.arith_shift_right, 4095, OP.bitwise_and)
+        cp("ri", "rl" + key, T.RL[:, o:o + 256], T.RI[:])
+
+    def save_numbers(parity):
+        tt("i6 l0", "l20", lf(20), li(6), lf(0), OP.subtract)
+        tt("l20 l18", "l21", lf(21), lf(20), lf(18), OP.mult)
+        tt("l21 l0", "l0", lf(0), lf(21), lf(0), OP.add)
+        tt("l18 l10", "l22", lf(22), lf(18), lf(10), OP.add)
+        tt("l15 l1", "l23", lf(23), lf(15), lf(1), OP.subtract)
+        tt("l23 l22", "l24", lf(24), lf(23), lf(22), OP.mult)
+        tt("l24 l1", "l1", lf(1), lf(24), lf(1), OP.add)
+        if parity:
+            cp("p2", "i12", li(12), T.P2[:, 256:272])
+            ts("i12", "i13", li(13), li(12), 1, OP.bitwise_and)
+            ts("i13", "thr", lf(3), li(13), -1.0, OP.mult, 8.0, OP.add)
+
+    def sv_payload():
+        tt("p0 thb", "sv", T.SV[:], D, T.THB[:], OP.is_le)
+        mms("sv idb", "p7", [(T.P7[:, 0], T.IDB[:], T.SV[:], False, True)])
+
+    sent = 0
+    EQ, T2 = T.P5[:, 0:256], T.P5[:, 256:512]
+    M1, M2 = T.P6[:, 0:256], T.P6[:, 256:512]
+    for t in range(RO):
+        F = T["F%d" % t]
+        fo, fg, fs = "f%do" % t, "f%dg" % t, "f%ds" % t
+        last = t == RO - 1
+        if t == 0:
+            tt("skv sl bg", "cg", T.CG[:], T.SKV[:].indirect(T.SL[:]), T.BG[:], OP.add)
+            tt(fo + " " + fg + " fl cg", "xig", T.XI[:, 0:256], F[:, 0:512].indirect(T.FL[:]), T.CG[:], OP.max)
+        else:
+            cp(fs, "sl", T.SL[:], F[:, 512:528])
+            tt("skv sl bia", "cg", T.CG[:], T.SKV[:].indirect(T.SL[:]), T.BIA[:], OP.add)
+            tt("cg " + fg, "xig", T.XI[:, 0:256], T.CG[:], F[:, 256:512], OP.max)
+        recs(0, "g")
+        for j, (a, b) in enumerate(PARTS):
+            act(XRK + "rlg", "u%d" % j, T.U[:, 256 * a:256 * b], T.XR[:].indirect(T.RL[:, 16 * a:16 * b]))
+        if t == 0:
+            tt("skv cl iot", "cc", T.CC[:], T.SKV[:].indirect(T.CL[:]), T.IOT[:], OP.add)
+            tt("cc " + fo, "xc", T.XC[:], T.CC[:], F[:, 0:256], OP.max)
+            ts(fo, "eq", EQ, F[:, 0:256], -2.0, OP.mult, NEG, OP.add)
+        else:
+            tt("hl cc " + fo + " " + fg, "xc", T.XC[:], F[:, 0:512].indirect(T.HL[:]), T.CC[:], OP.max)
+        ts("xig", "mg", T.MG[:], T.XI[:, 0:256], B - 1, OP.bitwise_and)
+        tt("eq mg", "t2", T2, EQ, T.MG[:], OP.min)
+        tt("t2 xc", "xic", T.XI[:, 256:512], T2, T.XC[:], OP.max)
+        recs(256, "c")
+        if t == 0:
+            th_tables()
+        mms("oneb kb", "p0", [(T.P0[:, 0], T.ONEB[0:1, 0:128], T.KB[0:1, :], True, False)])
+        cp("xig xic", "xf", T.XF[:], T.XI[:])
+        run("v", V.transpose, "xf", "xt", T.XT[:], T.XF[:])
+        for j, p in ((0, "P1"), (1, "P7")):
+            mms("xt swp", p.lower(), [(T[p][:, 0, :, u, :], T.SWP[:, 256 * u + 128 * gl:256 * u + 128 * gl + 128], T.XT[:, 8 * j:8 * j + 8, gl, :],
+                                       u + gl == 0, j == 0 and u + gl == 2) for u in range(2) for gl in range(2)])
+        for j, (a, b) in enumerate(PARTS):
+            tt(XRK + "rlc u%d" % j, "db%d" % j, T.DB[:, 256 * a:256 * b], T.XR[:].indirect(T.RL[:, 256 + 16 * a:256 + 16 * b]),
+               T.U[:, 256 * a:256 * b], OP.subtract)
+            act("db%d" % j, "ab%d" % j, T.AB[:, a:b], T.DB[:, 256 * a:256 * b], AF.Abs)
+        for j, (a, b, need) in enumerate(SUMS):
+            mms(need + " sq", "p0", [(T.P0[:, 0, a:b, :], T.SQ[:, 128 * q:128 * q + 128], T.AB[:, a:b, q, :], False, j == len(SUMS) - 1 and q == 15)
+                                     for q in range(16)])
+        ts("xic", "flg", T.FLG[:], T.XI[:, 256:512], float(B), OP.is_ge, NEG, OP.mult)
+        tt("t2 flg", "eq", EQ, T2, T.FLG[:], OP.add)
+        tt("eq mk", "ya", T.YA[:], EQ, T.MK[:], OP.max)
+        if t:
+            save_numbers(True)
+        new_saved_clause()
+        D = T.P0[:, 0]
+        tt("p0 tha", "nov", T.NOV[:], D, T.THA[:], OP.is_le)
+        run("v", V.tensor_tensor_scan, "rst0 nov", "ns", T.NS[:], T.RST[:, 0:256], T.NOV[:], 0.0, OP.mult, OP.add)
+        tt("ns thr", "l8", lf(8), T.NS[:, 15::16], lf(3), OP.is_gt)
+        ts("l8", "l9", lf(9), lf(8), -2.0 * NEG, OP.mult, NEG, OP.add)
+        tt("l9 bcc diag", "ex", T.EX[:], lf(9).indirect(T.BCC[:]), T.DIAG[:], OP.mult)
+        mms("ex blkb", "p2", [(T.P2[:, 0:256], T.BLKB[:], T.EX[:], True, True)])
+        tt("p0 nov", "ky", T.KY[:], D, T.NOV[:], OP.mult)
+        run("v", V.tensor_tensor_scan, "rst0 ky", "km", T.KM[:], T.RST[:, 0:256], T.KY[:], 0.0, OP.mult, OP.max)
+        tt("ns thr", "l10", lf(10), T.NS[:, 15::16], lf(3), OP.is_le)
+        tt("km bc15 ky", "mask", T.MASK[:], T.KM[:].indirect(T.BC15[:]), T.KY[:], OP.is_equal)
+        tt("l10 l0", "l11", lf(11), lf(10), lf(0), OP.mult)
+        tt("p1 mask", "mx0", T.MX[:, 0:256], T.P1[:, 0], T.MASK[:], OP.mult)
+        if last:
+            sv_payload()
+        run("v", V.tensor_tensor_scan, "rst0 mx0", "sc0", T.SC[:, 0:256], T.RST[:, 0:256], T.MX[:, 0:256], 0.0, OP.mult, OP.add)
+        tt("p2 ya", "m1", M1, T.P2[:, 0:256], T.YA[:], OP.min)
+        tt("sc0 l8", "l12", lf(12), T.SC[:, 15:256:16], lf(8), OP.mult)
+        tt("m1 base", fo, F[:, 0:256], M1, T.BASE[:], OP.max)
+        tt("l12 l11", "i6", li(6), lf(12), lf(11), OP.add)
+        if not last:
+            ts("i6", "i7", li(7), li(6), 1023, OP.bitwise_and)
+            ts("i6", "i8", li(8), li(6), 10, OP.arith_shift_right, 2047, OP.bitwise_and)
+            ts("i7", "fl", T.FL[:], li(7), -16.0, OP.add)
+            C = T["COL%d" % t]
+            ts("i8", "cols", C[:, 256:272], li(8), -592.0, OP.add)
+            cp("fl " + fo + " " + fg, "col", C[:, 0:256], F[:, 0:512].indirect(T.FL[:]))
+            d = 1 + t % (N - 1)
+            dst = T.cores[(rank + d) % N]
+            rel = routes(topo, core, dst)
+            before("gc", ["cols", "col"], [])
+            if rel:
+                w = 272 // len(rel)
+                tr = []
+                for k, c in enumerate(rel):
+                    rid, pid = topo.addr(c, core)
+                    es = topo.engines(core, c)
+                    tr.append(RemoteDMATransfer(dst_ids=[DstId(rid=rid, pnc=pid)], dma_engine_mask=only(es[4 * k:], 4),
+                                                remote_sem=T.sem["in%d" % t], src=C[:, k * w:(k + 1) * w], dst=T["RB%d" % t][:, 0:w]))
+                g.remote_dma_fused(tr, local_sem=T.sem.sent)
+                sent += 4 * len(rel)
+            else:
+                rid, pid = topo.addr(dst, core)
+                g.remote_dma(T["F%d" % (t + 1)][:, 256:528], C[:], T.sem["arr%d" % t], T.sem.sent, pid, rid, topo.mask(core, dst))
+                sent += len(topo.engines(core, dst))
+            src = T.cores[(rank - d) % N]
+            rin = routes(topo, src, core)
+            n = sum(len(topo.engines(c, core)) for c in rin) if rin else len(topo.engines(src, core))
+            arrive("arr%d" % t, n, "f%dg f%ds" % (t + 1, t + 1))
+            sv_payload()
+        tt("p7 mask", "mx1", T.MX[:, 256:512], T.P7[:, 0], T.MASK[:], OP.mult)
+        run("v", V.tensor_tensor_scan, "rst1 mx1", "sc1", T.SC[:, 256:512], T.RST[:, 256:512], T.MX[:, 256:512], 0.0, OP.mult, OP.add)
+        tt("l10 l4", "l13", lf(13), lf(10), lf(4), OP.mult)
+        tt("sc1 l8", "l14", lf(14), T.SC[:, 271::16], lf(8), OP.mult)
+        tt("l13 l14", "i9", li(9), lf(13), lf(14), OP.add)
+        ts("i9", "i10", li(10), li(9), 10, OP.arith_shift_right, 2047, OP.bitwise_and)
+        ts("i9", "i11", li(11), li(9), 1023, OP.bitwise_and)
+        ts("i10", "l15", lf(15), li(10), -592.0, OP.add)
+        ts("i11", "l16", lf(16), li(11), -16.0, OP.add)
+        if not last:
+            tt("l16 bcc diag", "eh", T.EH[:], lf(16).indirect(T.BCC[:]), T.DIAG[:], OP.mult)
+            mms("eh blkf", "p4", [(T.P4[:, 0:256], T.BLKF[:], T.EH[:], True, True)])
+            act("p4", "bh", T.BH[:], T.P4[:, 0:256])
+            act(fo, "f%do" % (t + 1), T["F%d" % (t + 1)][:, 0:256], F[:, 0:256])
+            cp("l15", "cl", T.CL[:], lf(15))
+            cp("l16", "hl", T.HL[:], lf(16))
+        ts("sc1", "l17", lf(17), T.SC[:, 271::16], float(2 * B), OP.is_ge)
+        tt("l17 l8", "l18", lf(18), lf(17), lf(8), OP.mult)
+        ts("l18", "l19", lf(19), lf(18), -2.0 * NEG, OP.mult, NEG, OP.add)
+        tt("l19 bcc diag", "ev", T.EV[:], lf(19).indirect(T.BCC[:]), T.DIAG[:], OP.mult)
+        if last:
+            mms("ev nblk", "p3", [(T.P3[:, 256:512], T.NBLK[:], T.EV[:], True, True)])
+        else:
+            mms("ev blkb nblk", "p3", [(T.P3[:, 0:256], T.BLKB[:], T.EV[:], True, True), (T.P3[:, 256:512], T.NBLK[:], T.EV[:], True, True)])
+            tt("skv cl bh", "cc", T.CC[:], T.SKV[:].indirect(T.CL[:]), T.BH[:], OP.add)
+            tt("p4 iot", "xc", T.XC[:], T.P4[:, 0:256], T.IOT[:], OP.is_equal)
+            tt("xc " + fo, "flg", T.FLG[:], T.XC[:], F[:, 0:256], OP.mult)
+            ts("flg", "eq", EQ, T.FLG[:], -2.0, OP.mult, NEG, OP.add)
+        if not last:
+            act("l8", "sb", T.SB[:], lf(8))
+            mms("sb diag", "p2", [(T.P2[:, 256:272], T.DIAG[:, 0:128], T.SB[:], True, True)])
+            act("m1", "ya", T.YA[:], M1)
+            tt("p3 ya", "m2", M2, T.P3[:, 0:256], T.YA[:], OP.min)
+            tt("p3 ya", "mk", T.MK[:], T.P3[:, 256:512], T.YA[:], OP.min)
+            tt("m2 base", "base", T.BASE[:], M2, T.BASE[:], OP.max)
+    save_numbers(False)
+    F = T.F3
+    cp("f3o", "pi", T.PI[:], F[:, 0:256])
+    ts("pi", "qi", T.QI[:], T.PI[:], 1023, OP.bitwise_and)
+    ts("f3o", "m2", M2, F[:, 0:256], -606240.0, OP.add)
+    cp("m1", "ya", T.YA[:], M1)
+    tt("m2 qi", "yo", T.YO[:], M2, T.QI[:], OP.add)
+    tt("p3 ya", "m2", M2, T.P3[:, 256:512], T.YA[:], OP.min)
+    ts("m2", "p2", T.P2[:, 0:256], M2, 0.0, OP.is_ge)
+    ts("yo", "ym", T.YM[:], T.YO[:], -1.0, OP.max)
+    tt("p2 ym", "yo", T.YO[:], T.P2[:, 0:256], T.YM[:], OP.add)
+    load("sync", T.yf[:], T.YO[:], "out", "yf", "yo")
+
+    def number(key, src, j):
+        ts(key, "n1", li(14), src, 10, OP.arith_shift_right, 2047, OP.bitwise_and)
+        ts(key, "n2", li(15), src, 1023, OP.bitwise_and)
+        ts("n1", "n3", lf(25), li(14), 512.0, OP.mult, float(-592 * 512 - 16), OP.add)
+        for k in range(2):
+            tt("n3 n2", "fld", T.FLD[:, 32 * j + 16 * k:32 * j + 16 * k + 16], lf(25), li(15), OP.add)
+    number("i6", li(6), 0)
+    number("i9", li(9), 1)
+    cp("l0", "i0", li(0), lf(0))
+    number("i0", li(0), 2)
+    for k in range(2):
+        cp("l1", "fld", T.FLD[:, 96 + 16 * k:112 + 16 * k], lf(1))
+    run("v", V.transpose, "fld", "flt", T.FLT[:], T.FLD[:])
+    for j, y in enumerate((T.yg, T.yc, T.ysg, T.yk)):
+        ts("flt mu0", "fo%d" % j, T.FO[:, 16 * j:16 * j + 16], T.FLT[:, 32 * j:32 * j + 16], T.MU0[:, 0:1], OP.mult)
+        ts("flt mu1", "fp%d" % j, T.FP[:, 16 * j:16 * j + 16], T.FLT[:, 32 * j + 16:32 * j + 32], T.MU1[:, 0:1], OP.mult)
+        tt("fo%d fp%d" % (j, j), "fq%d" % j, T.FO[:, 16 * j:16 * j + 16], T.FO[:, 16 * j:16 * j + 16], T.FP[:, 16 * j:16 * j + 16], OP.add)
+        load("sync", y[:], T.FO[:, 16 * j:16 * j + 16], "out", "y%d" % j, "fq%d" % j)
+    g.sync.wait_ge(T.sem.out, cnt["out"])
+    g.wait_ge(T.sem.sent, sent)
+    for q in ("v", "s", "pe", "gc"):
+        g.sync.wait_ge(T.sem[q], cnt[q])
+    for s in LOADS:
+        if not any(k[1] == s for k in seen):
+            g.sync.wait_ge(T.sem[s], 16)

@@ -7,64 +7,64 @@ NEG = -8388608.0
 B = 1 << 21
 KE = 592 * 1024 + 16
 PARTS = [(0, 4), (4, 8), (8, 12), (12, 14), (14, 16)]
-SUMS = [(0, 8, "ab0 ab1"), (8, 12, "ab2"), (12, 16, "ab3 ab4")]
+SUMS = [(0, 4, "ab0"), (4, 8, "ab1"), (8, 12, "ab2"), (12, 16, "ab3 ab4")]
+HOP = 8
 LOADS = ["l_gs0", "l_gs1", "l_gf0", "l_gf1", "l_gc0", "l_gc1", "l_gfr", "l_fr", "l_sk", "l_th", "l_x0", "l_x1"]
 
+
+def f32(*s):
+    return ("sbuf", [128] + list(s), "float32")
+
+
+def i32(*s):
+    return ("sbuf", [128] + list(s), "int32")
+
+
+def b16(*s):
+    return ("sbuf", [128] + list(s), "bfloat16")
+
+
+def u16(*s):
+    return ("sbuf", [128] + list(s), "uint16")
+
+
 SCRATCH = {
-    "XR": ("sbuf", [128, 4096], "bfloat16"),
-    "SKI": ("sbuf", [128, 1024], "int32"), "SKU": ("sbuf", [128, 1024], "float32"), "SKV": ("sbuf", [128, 1024], "float32"),
-    "FRI": ("sbuf", [128, 256], "int32"), "FRQ": ("sbuf", [128, 256], "int32"), "OW": ("sbuf", [128, 256], "float32"),
-    "BASE": ("sbuf", [128, 256], "float32"), "MK": ("sbuf", [128, 256], "float32"), "YA": ("sbuf", [128, 256], "float32"),
-    "FLG": ("sbuf", [128, 256], "float32"),
-    "F0": ("sbuf", [128, 528], "float32"), "F1": ("sbuf", [128, 528], "float32"),
-    "F2": ("sbuf", [128, 528], "float32"), "F3": ("sbuf", [128, 528], "float32"),
-    "COL0": ("sbuf", [128, 272], "float32"), "COL1": ("sbuf", [128, 272], "float32"), "COL2": ("sbuf", [128, 272], "float32"),
-    "RB0": ("sbuf", [128, 68], "float32"), "RB2": ("sbuf", [128, 68], "float32"),
-    "TT": ("sbuf", [128, 96], "int32"), "TX": ("sbuf", [128, 96], "int32"), "TA": ("sbuf", [128, 48], "float32"),
-    "TB": ("sbuf", [128, 48], "float32"), "TL": ("sbuf", [128, 48], "float32"),
-    "GFR": ("sbuf", [8, 256], "int32"), "GFB": ("sbuf", [8, 256], "bfloat16"),
-    "THI": ("sbuf", [128, 1], "int32"), "THF": ("sbuf", [128, 1], "float32"), "THD": ("sbuf", [128, 256], "float32"),
-    "THA": ("sbuf", [128, 256], "float32"), "THB": ("sbuf", [128, 256], "float32"), "THW": ("sbuf", [128, 256], "int32"),
-    "ONEB": ("sbuf", [128, 256], "bfloat16"), "ONEF": ("sbuf", [128, 128], "float32"),
-    "R16": ("sbuf", [16, 256], "bfloat16"), "R8": ("sbuf", [8, 128], "bfloat16"),
-    "IDF": ("sbuf", [128, 128], "float32"), "IDB": ("sbuf", [128, 128], "bfloat16"),
-    "BLKB": ("sbuf", [128, 128], "bfloat16"), "NBLK": ("sbuf", [128, 128], "bfloat16"), "BLKF": ("sbuf", [128, 128], "float32"),
-    "DIAG": ("sbuf", [128, 256], "bfloat16"), "SQ": ("sbuf", [128, 2048], "bfloat16"), "SWP": ("sbuf", [128, 512], "float32"),
-    "KB": ("sbuf", [128, 256], "bfloat16"), "RST": ("sbuf", [128, 512], "bfloat16"),
-    "IOT": ("sbuf", [128, 256], "float32"), "BIA": ("sbuf", [128, 256], "float32"), "BG": ("sbuf", [128, 256], "float32"),
-    "BH": ("sbuf", [128, 256], "float32"),
-    "C16": ("sbuf", [128, 16], "float32"), "PIO": ("sbuf", [128, 16], "int32"), "PM": ("sbuf", [128, 16], "int32"),
-    "LIK": ("sbuf", [128, 16], "float32"), "MUI": ("sbuf", [128, 16], "int32"), "MU1": ("sbuf", [128, 16], "float32"), "MU0": ("sbuf", [128, 16], "float32"),
-    "BC15": ("sbuf", [128, 16], "uint16"), "BCC": ("sbuf", [128, 16], "uint16"),
-    "SL": ("sbuf", [128, 16], "uint16"), "FL": ("sbuf", [128, 16], "uint16"), "CL": ("sbuf", [128, 16], "uint16"), "HL": ("sbuf", [128, 16], "uint16"),
-    "CG": ("sbuf", [128, 256], "float32"), "CC": ("sbuf", [128, 256], "float32"), "XC": ("sbuf", [128, 256], "float32"), "MG": ("sbuf", [128, 256], "int32"),
-    "XI": ("sbuf", [128, 512], "int32"), "PI": ("sbuf", [128, 256], "int32"), "QI": ("sbuf", [128, 256], "int32"),
-    "ZI": ("sbuf", [128, 256], "int32"), "RI": ("sbuf", [128, 256], "int32"), "RL": ("sbuf", [128, 512], "uint16"),
-    "U": ("sbuf", [128, 4096], "bfloat16"), "DB": ("sbuf", [128, 4096], "bfloat16"),
-    "AB": ("sbuf", [128, 16, 16, 16], "bfloat16"),
-    "XF": ("sbuf", [128, 512], "float32"), "XT": ("sbuf", [128, 16, 2, 16], "float32"),
-    "NOV": ("sbuf", [128, 256], "bfloat16"), "NS": ("sbuf", [128, 256], "bfloat16"), "SV": ("sbuf", [128, 256], "bfloat16"),
-    "SB": ("sbuf", [128, 16], "bfloat16"), "KY": ("sbuf", [128, 256], "float32"), "KM": ("sbuf", [128, 256], "float32"), "MASK": ("sbuf", [128, 256], "bfloat16"),
-    "MX": ("sbuf", [128, 512], "float32"), "SC": ("sbuf", [128, 512], "float32"),
-    "EX": ("sbuf", [128, 256], "bfloat16"), "EV": ("sbuf", [128, 256], "bfloat16"), "EH": ("sbuf", [128, 256], "float32"),
-    "LF": ("sbuf", [128, 512], "float32"), "LI": ("sbuf", [128, 256], "int32"),
-    "FLD": ("sbuf", [128, 128], "float32"), "FLT": ("sbuf", [128, 128], "float32"), "FO": ("sbuf", [128, 64], "float32"), "FP": ("sbuf", [128, 64], "float32"),
-    "YO": ("sbuf", [128, 256], "float32"), "YM": ("sbuf", [128, 256], "float32"),
+    "XR": b16(4096), "SKI": i32(1024), "SKU": f32(1024), "SKV": f32(1024), "FRI": i32(256), "FRQ": i32(256), "OW": f32(256),
+    "BASE": f32(256), "MK": f32(256), "YA": f32(256), "FLG": f32(256), "F0": f32(528), "F1": f32(528), "F2": f32(528), "F3": f32(528),
+    "COL0": f32(272), "COL1": f32(272), "COL2": f32(272), "RB0": f32(136), "RB2": f32(136),
+    "TT": i32(96), "TX": i32(3, 2, 16), "TA": f32(3, 16), "TB": f32(3, 16), "TL": f32(3, 16),
+    "GFR": ("sbuf", [8, 256], "int32"), "GFB": ("sbuf", [8, 256], "bfloat16"), "R16": ("sbuf", [16, 256], "bfloat16"), "R8": ("sbuf", [8, 128], "bfloat16"),
+    "THI": i32(1), "THF": f32(1), "THD": f32(256), "THA": f32(256), "THB": f32(256), "THW": i32(256),
+    "ONEB": b16(256), "ONEF": f32(4, 2, 16), "ONEG": f32(128), "IDF": f32(128), "IDB": b16(128),
+    "BLKF": f32(128), "BLKH": ("sbuf", [128, 128], "float16"), "NPR": ("sbuf", [1, 512], "bfloat16"),
+    "ONEH": ("sbuf", [1, 128], "float16"), "NIH": ("sbuf", [1, 256], "float16"),
+    "DIAG": b16(256), "DIF": f32(16), "SQ": b16(2048), "TQ": b16(2048), "SWP": f32(4, 4, 2, 16),
+    "KB": b16(256), "RST": b16(512), "IOT": f32(256), "BIA": f32(256), "BG": f32(256),
+    "C16": f32(16), "PIO": i32(16), "PM": i32(16), "LIK": f32(16), "MUI": i32(16), "MU1": f32(16), "MU0": f32(16),
+    "BC15": u16(16), "SL": u16(16), "FL": u16(16), "CL": u16(16), "HL": u16(16), "BCC": u16(16),
+    "CG": f32(256), "VC": f32(256), "WC": f32(256), "XC": f32(256), "MG": i32(256),
+    "XI": i32(512), "PI": i32(512), "QI": i32(512), "ZI": i32(512), "RI": i32(512), "RL": u16(512),
+    "U": b16(4096), "DB": b16(4096), "AB": b16(16, 16, 16), "XF": f32(512), "XT": f32(16, 2, 16),
+    "NOV": b16(256), "NS": b16(256), "SV": b16(256), "SB": b16(16), "S2": b16(2, 16), "KY": f32(256), "KM": f32(256), "MASK": b16(256),
+    "MX": f32(512), "SC": f32(512), "EH": ("sbuf", [128, 256], "float16"), "HA": f32(256), "WN": f32(256),
+    "LF": f32(512), "LI": i32(256), "SAV": i32(32),
+    "FLD": f32(128), "FLT": f32(4, 2, 16), "FO": f32(4, 16), "FP": f32(4, 16), "YO": f32(256), "YM": f32(256),
     "P0": ("psum", [128, 2, 16, 16], "float32"), "P1": ("psum", [128, 2, 8, 2, 16], "float32"), "P2": ("psum", [128, 512], "float32"),
-    "P3": ("psum", [128, 512], "float32"), "P4": ("psum", [128, 512], "float32"), "P5": ("psum", [128, 512], "float32"),
+    "P3": ("psum", [128, 2, 16, 16], "float32"), "P4": ("psum", [128, 512], "float32"), "P5": ("psum", [128, 512], "float32"),
     "P6": ("psum", [128, 512], "float32"), "P7": ("psum", [128, 2, 8, 2, 16], "float32"),
 }
-SEMAPHORES = LOADS + ["v", "s", "pe", "gc", "out", "sent", "in0", "in2", "arr0", "arr1", "arr2"]
+SEMAPHORES = LOADS + ["v", "s", "pe", "gq", "out", "sent", "in0", "in2", "arr0", "arr1", "arr2"]
 
 
 def routes(topo, a, b):
     if topo.may_write(a, b):
         return []
-    return [c for c in topo.cores_of(a) if c != a and topo.may_write(c, b)]
+    own = [c for c in topo.cores_of(a) if c != a and topo.may_write(c, b)]
+    return [[c for c in own if topo.die(c) == die][0] for die in sorted(set(topo.die(c) for c in own))]
 
 
-def only(m, n):
-    return sum(1 << e for e in m[:n])
+def only(engines, n):
+    return sum(1 << e for e in engines[:n])
 
 
 def relay(g, core, T, topo):
@@ -79,7 +79,7 @@ def relay(g, core, T, topo):
             if core not in rel:
                 continue
             k, w = rel.index(core), 272 // len(rel)
-            g.wait_ge(T.sem["in%d" % t], 4)
+            g.wait_ge(T.sem["in%d" % t], HOP)
             rid, pid = topo.addr(b, core)
             g.remote_dma(T["F%d" % (t + 1)][:, 256 + k * w:256 + (k + 1) * w], T["RB%d" % t][:, 0:w], T.sem["arr%d" % t], T.sem.sent,
                          pid, rid, topo.mask(core, b))
@@ -92,7 +92,8 @@ def rank_program(g, core, T, topo):
     rank = T.rank_of(core)
     if rank is None:
         return relay(g, core, T, topo)
-    ENG = {"v": g.vector, "s": g.scalar, "pe": g.tensor, "gc": g, "sync": g.sync}
+    ENG = {"v": g.vector, "s": g.scalar, "pe": g.tensor, "gq": g, "sync": g.sync}
+    V = g.vector
     cnt, seen, wr, rd = {}, {}, {}, {}
 
     def before(q, reads, writes):
@@ -134,8 +135,6 @@ def rank_program(g, core, T, topo):
             wr[k] = [("net", sem, n)]
             rd[k] = []
 
-    V = g.vector
-
     def tt(reads, w, out, a, b, op):
         run("v", V.tensor_tensor, reads, w, out, a, b, op)
 
@@ -148,11 +147,11 @@ def rank_program(g, core, T, topo):
     def cp(reads, w, out, a):
         run("v", V.tensor_copy, reads, w, out, a)
 
-    def act(reads, w, out, a, func=AF.Copy, scale=1.0):
-        if scale == 1.0:
-            run("s", g.scalar.activation, reads, w, out, a, func)
-        else:
-            run("s", g.scalar.activation, reads, w, out, a, func, scale=scale)
+    def scan(reads, w, out, d0, d1, op):
+        run("v", V.tensor_tensor_scan, reads, w, out, d0, d1, 0.0, OP.mult, op)
+
+    def act(reads, w, out, a, func=AF.Copy, **kw):
+        run("s", g.scalar.activation, reads, w, out, a, func, **kw)
 
     def mms(reads, w, calls):
         reads, w = reads.split(), w.split()
@@ -161,16 +160,19 @@ def rank_program(g, core, T, topo):
             ins = g.tensor.matmul(*c)
         after("pe", ins, "pe", 1, reads, w)
 
-    def lf(j):
-        return T.LF[:, 16 * j:16 * j + 16]
+    def lf(j, n=1):
+        return T.LF[:, 16 * j:16 * j + 16 * n]
 
-    def li(j):
-        return T.LI[:, 16 * j:16 * j + 16]
+    def li(j, n=1):
+        return T.LI[:, 16 * j:16 * j + 16 * n]
+
+    SG, SCL = T.SAV[:, 0:16], T.SAV[:, 16:32]
+    ONES = T.ONEB[0:1, 0:128]
 
     load("sync", T.TT[:, 0:16], T.gs[:], "l_gs0", "tt0")
     load("sync", T.TT[:, 16:32], T.gs[:], "l_gs1", "tt1")
-    load("sync", T.GFR[:], T.gf[:], "l_gfr", "gfr")
     load("sync", T.SKI[:], T.sk[:], "l_sk", "ski")
+    load("sync", T.GFR[:], T.gf[:], "l_gfr", "gfr")
     load("sync", T.XR[:, 592:4096], T.x[:, 0:3504], "l_x0", "xr0")
     load("s", T.TT[:, 32:48], T.gf[:], "l_gf0", "tt2")
     load("s", T.TT[:, 48:64], T.gf[:], "l_gf1", "tt3")
@@ -183,124 +185,130 @@ def rank_program(g, core, T, topo):
 
     run("v", V.memset, "", "oneb", T.ONEB[:], 1.0)
     run("v", V.memset, "", "onef", T.ONEF[:], 1.0)
-    sel = lambda o, i, p, r, w: run("gc", g.affine_select, r, w, o, i, p, OP.is_equal, 0.0, 0, 1)
-    iota = lambda o, p, base, cm, w: run("gc", g.iota, "", w, o, p, base, cm, allow_small_or_imprecise_dtypes=True)
+    run("v", V.memset, "", "oneg", T.ONEG[:], 1.0)
+
+    def sel(o, i, p, base, r, w):
+        run("gq", g.affine_select, r, w, o, i, p, OP.is_equal, 0.0, base, 1)
+
+    def iota(o, p, base, cm, w):
+        run("gq", g.iota, "", w, o, p, base, cm, allow_small_or_imprecise_dtypes=True)
     iota(T.C16[:], [[16, 16]], KE, 0, "c16")
     iota(T.PIO[:], [[0, 16]], 0, 1, "pio")
-    sel(T.R8[:], T.ONEB[0:8, 0:128], [[-1, 8], [0, 16]], "oneb", "r8")
-    sel(T.R16[:], T.ONEB[0:16, :], [[0, 16], [-1, 16]], "oneb", "r16")
+    sel(T.R8[:], T.ONEB[0:8, 0:128], [[-1, 8], [0, 16]], 0, "oneb", "r8")
+    sel(T.R16[:], T.ONEB[0:16, :], [[0, 16], [-1, 16]], 0, "oneb", "r16")
     iota(T.IOT[:], [[1, 256]], 0, 0, "iot")
-    sel(T.IDF[:], T.ONEF[:], [[-1, 128]], "onef", "idf")
     iota(T.KB[:], [[0, 16], [-1, 16]], 15, 0, "kb")
+    sel(T.IDF[:], T.ONEG[:], [[-1, 128]], 0, "oneg", "idf")
     iota(T.BIA[:], [[1, 256]], 256, 0, "bia")
-    for j in range(8):
-        act("iot", "sq", T.SQ[:, 256 * j:256 * j + 256], T.IOT[:], AF.Copy, 0.0)
-    for j in range(2):
-        act("iot", "swp", T.SWP[:, 256 * j:256 * j + 256], T.IOT[:], AF.Copy, 0.0)
     ts("pio", "pm", T.PM[:], T.PIO[:], 15, OP.bitwise_and)
     ts("pio", "mui", T.MUI[:], T.PIO[:], 4, OP.arith_shift_right, 1, OP.bitwise_and)
+    ts("c16", "bc15", T.BC15[:], T.C16[:], float(15 - KE), OP.add)
     cp("mui", "mu1", T.MU1[:], T.MUI[:])
     ts("mui", "mu0", T.MU0[:], T.MUI[:], -1.0, OP.mult, 1.0, OP.add)
     tt("pm c16", "lik", T.LIK[:], T.PM[:], T.C16[:], OP.add)
-    ts("c16", "bc15", T.BC15[:], T.C16[:], float(15 - KE), OP.add)
     ts("c16", "bcc", T.BCC[:], T.C16[:], float(-KE), OP.add, 0.0625, OP.mult)
     mms("r8", "p4", [(T.P4[:, 0:128], T.R8[:], T.R8[:], True, True)])
-    mms("r16", "p3", [(T.P3[:, 0:256], T.R16[:, 0:128], T.R16[:], True, True)])
+    mms("r16", "p0", [(T.P0[:, 0], T.R16[:, 0:128], T.R16[:], True, True)])
+    for j in range(8):
+        act("iot", "sq", T.SQ[:, 256 * j:256 * j + 256], T.IOT[:], scale=0.0)
+    for j in range(2):
+        act("iot", "swp", T.SWP[:, 2 * j:2 * j + 2], T.IOT[:], scale=0.0)
+    for u in range(2):
+        for gl in range(2):
+            sel(T.SWP[:, 2 * u + gl, :, gl, :], T.ONEF[:, :, 0, :], [[-32, 4], [-1, 16]], -16 * u, "onef swp", "sw%d" % (2 * u + gl))
 
     run("v", V.transpose, "tt0 tt1 tt2 tt3 tt4 tt5", "tx", T.TX[:], T.TT[:])
-    for j in range(3):
-        ts("tx mu0", "ta%d" % j, T.TA[:, 16 * j:16 * j + 16], T.TX[:, 32 * j:32 * j + 16], T.MU0[:, 0:1], OP.mult)
-        ts("tx mu1", "tb%d" % j, T.TB[:, 16 * j:16 * j + 16], T.TX[:, 32 * j + 16:32 * j + 32], T.MU1[:, 0:1], OP.mult)
-    tt("ta0 ta1 ta2 tb0 tb1 tb2", "tl", T.TL[:], T.TA[:], T.TB[:], OP.add)
-    cp("tl", "sl", T.SL[:], T.TL[:, 0:16])
-    cp("tl", "fl", T.FL[:], T.TL[:, 16:32])
-    cp("tl", "cl", T.CL[:], T.TL[:, 32:48])
-    ts("tl", "l2", lf(2), T.TL[:, 0:16], 1024.0, OP.mult, float(KE), OP.add)
-    tt("tl l2", "l0", lf(0), T.TL[:, 16:32], lf(2), OP.add)
-    cp("tl", "l1", lf(1), T.TL[:, 32:48])
+    ts("tx mu0", "ta", T.TA[:], T.TX[:, :, 0, :], T.MU0[:, 0:1], OP.mult)
+    ts("tx mu1", "tb", T.TB[:], T.TX[:, :, 1, :], T.MU1[:, 0:1], OP.mult)
+    ts("fri", "frq", T.FRQ[:], T.FRI[:], 511, OP.bitwise_and)
+    tt("ta tb", "tl", T.TL[:], T.TA[:], T.TB[:], OP.add)
     cp("gfr", "gfb", T.GFB[:], T.GFR[:])
     mms("r8 gfb", "p2", [(T.P2[:, 0:256], T.R8[:], T.GFB[:], True, True)])
     act("p2", "bg", T.BG[:], T.P2[:, 0:256])
-    ts("fri", "frq", T.FRQ[:], T.FRI[:], 511, OP.bitwise_and)
     ts("fri", "p6", T.P6[:, 0:256], T.FRI[:], 2.0, OP.mult, float(KE), OP.add)
     ts("fri", "p5", T.P5[:, 0:256], T.FRI[:], 0.0, OP.is_lt, NEG, OP.mult)
     tt("p6 frq", "ow", T.OW[:], T.P6[:, 0:256], T.FRQ[:], OP.subtract)
+    cp("tl", "sl", T.SL[:], T.TL[:, 0, :])
     tt("p5 ow", "f0o", T.F0[:, 0:256], T.P5[:, 0:256], T.OW[:], OP.add)
+    cp("tl", "fl", T.FL[:], T.TL[:, 1, :])
     act("f0o", "f0g", T.F0[:, 256:512], T.F0[:, 0:256])
-    act("f0o", "base", T.BASE[:], T.F0[:, 0:256])
-    ts("ski", "sku", T.SKU[:], T.SKI[:], 1024.0, OP.mult, float(KE + B), OP.add)
     for j, p in ((0, "P5"), (1, "P6")):
         cs = slice(512 * j, 512 * j + 512)
         ts("ski", p.lower(), T[p][:], T.SKI[:, cs], 1024.0, OP.is_ge, float(-(1 << 20) - 2 * B), OP.mult)
-        tt(p.lower() + " sku", "skv", T.SKV[:, cs], T[p][:], T.SKU[:, cs], OP.add)
-    wr["skv"] = [("v", "v", cnt["v"])]
+        ts("ski", "sku%d" % j, T.SKU[:, cs], T.SKI[:, cs], 1024.0, OP.mult, float(KE + B), OP.add)
+    for j, p in ((0, "P5"), (1, "P6")):
+        cs = slice(512 * j, 512 * j + 512)
+        tt("%s sku%d" % (p.lower(), j), "skv", T.SKV[:, cs], T[p][:], T.SKU[:, cs], OP.add)
+    cp("tl", "cl", T.CL[:], T.TL[:, 2, :])
+    act("p0", "diag", T.DIAG[:], T.P0[:, 0])
+    act("p4", "blkf", T.BLKF[:], T.P4[:, 0:128])
+    act("p0", "dif", T.DIF[:], T.P0[:, 0, 0, :], scale=-2.0 * NEG)
+    for q in range(16):
+        act("p4", "sq", T.SQ[:, 128 * q + q:128 * q + 128:16], T.P4[:, q:128:16], scale=16.0)
+    act("idf", "idb", T.IDB[:], T.IDF[:], scale=-NEG)
+    act("f0o", "base", T.BASE[:], T.F0[:, 0:256])
 
-    def late_constants():
-        act("p4", "blkb", T.BLKB[:], T.P4[:, 0:128])
-        act("p3", "diag", T.DIAG[:], T.P3[:, 0:256])
-        act("p4", "blkf", T.BLKF[:], T.P4[:, 0:128])
-        act("p4", "nblk", T.NBLK[:], T.P4[:, 0:128], AF.Copy, -1.0)
-        for q in range(16):
-            act("p4", "sq", T.SQ[:, 128 * q + q:128 * q + 128:16], T.P4[:, q:128:16], AF.Copy, 16.0)
-        for u in range(2):
-            for gl in range(2):
-                for a in range(4):
-                    o = 128 * (2 * u + gl) + 32 * a + 16 * gl
-                    act("idf", "swp", T.SWP[:, o:o + 16], T.IDF[:, 32 * a + 16 * u:32 * a + 16 * u + 16])
-        act("idf", "idb", T.IDB[:], T.IDF[:], AF.Copy, -NEG)
-    late_constants()
-
-    def th_tables():
+    def later_constants():
         cp("thi", "thf", T.THF[:], T.THI[:])
         ts("diag thf", "thd", T.THD[:], T.DIAG[:], T.THF[:, 0:1], OP.mult)
         mms("blkf thd", "p2", [(T.P2[:, 0:256], T.BLKF[:], T.THD[:], True, True)])
-        ts("p2", "thw", T.THW[:], T.P2[:, 0:256], -1.0, OP.add)
-        ts("p2", "tha", T.THA[:], T.P2[:, 0:256], 16.0, OP.mult, 15.0, OP.add)
-        ts("thw", "thx", T.THW[:], T.THW[:], 1, OP.arith_shift_right)
-        ts("thx", "thb", T.THB[:], T.THW[:], 16.0, OP.mult, 15.0, OP.add)
         ts("kb", "rst0", T.RST[:, 0:256], T.KB[:], 15.0, OP.is_lt)
         ts("kb", "rst1", T.RST[:, 256:512], T.KB[:], 15.0, OP.is_lt)
         run("v", V.memset, "", "thr", lf(3), 8.0)
         run("v", V.memset, "", "mk", T.MK[:], NEG)
+        ts("tl", "l2", lf(2), T.TL[:, 0, :], 1024.0, OP.mult, float(KE), OP.add)
+        run("v", V.memset, "", "npr", T.NPR[:, 0:256], NEG)
+        run("v", V.memset, "", "npr", T.NPR[:, 256:512], -NEG)
+        cp("tl", "sav", SCL, T.TL[:, 2, :])
+        tt("tl l2", "sav", SG, T.TL[:, 1, :], lf(2), OP.add)
+        ts("p2", "thw", T.THW[:], T.P2[:, 0:256], -1.0, OP.add)
+        ts("p2", "tha", T.THA[:], T.P2[:, 0:256], 16.0, OP.mult, 15.0, OP.add)
+        ts("thw", "thw", T.THW[:], T.THW[:], 1, OP.arith_shift_right)
+        ts("thw", "thb", T.THB[:], T.THW[:], 16.0, OP.mult, 15.0, OP.add)
+        cp("blkf", "blkh", T.BLKH[:], T.BLKF[:])
+        cp("oneb", "oneh", T.ONEH[:], T.ONEB[0:1, 0:128])
+        ts("iot", "nih", T.NIH[:], T.IOT[0:1, :], -1.0, OP.mult)
+        new_saved_clause()
 
     def new_saved_clause():
-        cp("l0", "i0", li(0), lf(0))
-        ts("i0", "i1", li(1), li(0), 10, OP.arith_shift_right, 2047, OP.bitwise_and)
-        ts("i1", "l5", lf(5), li(1), -592.0, OP.add)
-        tt("l5 l1", "i2", li(2), lf(5), lf(1), OP.mult)
-        ts("i2", "i3", li(3), li(2), 5, OP.arith_shift_right)
-        ts("l1", "l6", lf(6), lf(1), 1.0, OP.add)
-        tt("i3 l6", "i4", li(4), li(3), lf(6), OP.add)
-        ts("i4", "i5", li(5), li(4), 1023, OP.bitwise_and)
+        ts("sav", "i1", li(1), SG, 10, OP.arith_shift_right, 2047, OP.bitwise_and)
+        ts("i1", "l5", lf(5), li(1), -560.0, OP.add)
+        tt("l5 sav", "l6", lf(6), lf(5), SCL, OP.mult)
+        ts("l6", "i2", li(2), lf(6), 32.0, OP.add)
+        ts("i2", "i5", li(5), li(2), 5, OP.arith_shift_right, 1023, OP.bitwise_and)
         ts("i5", "l7", lf(7), li(5), 1024.0, OP.mult)
         tt("l7 lik", "l4", lf(4), lf(7), T.LIK[:], OP.add)
 
-    def recs(o, key):
-        X = T.XI[:, o:o + 256]
-        ts("xi" + key, "pi", T.PI[:], X, 10, OP.arith_shift_right, 2047, OP.bitwise_and)
-        ts("xi" + key, "qi", T.QI[:], X, 1023, OP.bitwise_and)
-        tt("pi qi", "zi", T.ZI[:], T.PI[:], T.QI[:], OP.mult)
-        ts("zi", "ri", T.RI[:], T.ZI[:], 4, OP.arith_shift_right, 4095, OP.bitwise_and)
-        cp("ri", "rl" + key, T.RL[:, o:o + 256], T.RI[:])
+    def recs(o, n, key):
+        c = slice(o, o + n)
+        ts("xi" + key, "pi" + key, T.PI[:, c], T.XI[:, c], 10, OP.arith_shift_right, 2047, OP.bitwise_and)
+        ts("xi" + key, "qi" + key, T.QI[:, c], T.XI[:, c], 1023, OP.bitwise_and)
+        tt("pi%s qi%s" % (key, key), "zi" + key, T.ZI[:, c], T.PI[:, c], T.QI[:, c], OP.mult)
+        ts("zi" + key, "ri" + key, T.RI[:, c], T.ZI[:, c], 4, OP.arith_shift_right, 4095, OP.bitwise_and)
+        cp("ri" + key, "rl" + key, T.RL[:, c], T.RI[:, c])
 
     def save_numbers(parity):
-        tt("i6 l0", "l20", lf(20), li(6), lf(0), OP.subtract)
-        tt("l20 l18", "l21", lf(21), lf(20), lf(18), OP.mult)
-        tt("l21 l0", "l0", lf(0), lf(21), lf(0), OP.add)
-        tt("l18 l10", "l22", lf(22), lf(18), lf(10), OP.add)
-        tt("l15 l1", "l23", lf(23), lf(15), lf(1), OP.subtract)
-        tt("l23 l22", "l24", lf(24), lf(23), lf(22), OP.mult)
-        tt("l24 l1", "l1", lf(1), lf(24), lf(1), OP.add)
+        tt("l18 l10", "l22", lf(19), lf(18), lf(10), OP.add)
+        tt("i6 i7 sav", "l20", lf(20, 2), li(6, 2), T.SAV[:], OP.subtract)
         if parity:
             cp("p2", "i12", li(12), T.P2[:, 256:272])
+        tt("l20 l18 l22", "l21", lf(22, 2), lf(20, 2), lf(18, 2), OP.mult)
+        if parity:
             ts("i12", "i13", li(13), li(12), 1, OP.bitwise_and)
+        tt("l21 sav", "sav", T.SAV[:], lf(22, 2), T.SAV[:], OP.add)
+        if parity:
             ts("i13", "thr", lf(3), li(13), -1.0, OP.mult, 8.0, OP.add)
+
+    def swap(p, j, stop):
+        mms("xt sw0 sw1 sw2 sw3", p.lower(), [(T[p][:, 0, :, u, :], T.SWP[:, 2 * u + gl], T.XT[:, 8 * j:8 * j + 8, gl, :],
+                                               u + gl == 0, stop and u + gl == 2) for u in range(2) for gl in range(2)])
 
     def sv_payload():
         tt("p0 thb", "sv", T.SV[:], D, T.THB[:], OP.is_le)
         mms("sv idb", "p7", [(T.P7[:, 0], T.IDB[:], T.SV[:], False, True)])
 
     sent = 0
+    D = T.P0[:, 0]
     EQ, T2 = T.P5[:, 0:256], T.P5[:, 256:512]
     M1, M2 = T.P6[:, 0:256], T.P6[:, 256:512]
     for t in range(RO):
@@ -309,32 +317,36 @@ def rank_program(g, core, T, topo):
         last = t == RO - 1
         if t == 0:
             tt("skv sl bg", "cg", T.CG[:], T.SKV[:].indirect(T.SL[:]), T.BG[:], OP.add)
-            tt(fo + " " + fg + " fl cg", "xig", T.XI[:, 0:256], F[:, 0:512].indirect(T.FL[:]), T.CG[:], OP.max)
         else:
+            act(fg, "p3", T.P3[:, 0], F[:, 256:512])
+            act("hl " + fo + " " + fg, "wc", T.WC[:], F[:, 0:512].indirect(T.HL[:]))
             cp(fs, "sl", T.SL[:], F[:, 512:528])
             tt("skv sl bia", "cg", T.CG[:], T.SKV[:].indirect(T.SL[:]), T.BIA[:], OP.add)
-            tt("cg " + fg, "xig", T.XI[:, 0:256], T.CG[:], F[:, 256:512], OP.max)
-        recs(0, "g")
+        for k in range(2):
+            c = slice(128 * k, 128 * k + 128)
+            if t == 0:
+                tt(fo + " " + fg + " fl cg", "xig%d" % k, T.XI[:, c], F[:, 0:512].indirect(T.FL[:, 8 * k:8 * k + 8]), T.CG[:, c], OP.max)
+            else:
+                tt("cg p3", "xig%d" % k, T.XI[:, c], T.P3[:, 0, 8 * k:8 * k + 8, :], T.CG[:, c], OP.max)
+            recs(128 * k, 128, "g%d" % k)
         for j, (a, b) in enumerate(PARTS):
-            act(XRK + "rlg", "u%d" % j, T.U[:, 256 * a:256 * b], T.XR[:].indirect(T.RL[:, 16 * a:16 * b]))
+            act(XRK + "rlg%d" % (a // 8), "u%d" % j, T.U[:, 256 * a:256 * b], T.XR[:].indirect(T.RL[:, 16 * a:16 * b]))
         if t == 0:
-            tt("skv cl iot", "cc", T.CC[:], T.SKV[:].indirect(T.CL[:]), T.IOT[:], OP.add)
-            tt("cc " + fo, "xc", T.XC[:], T.CC[:], F[:, 0:256], OP.max)
+            for q in range(16):
+                act("p4 dif", "tq", T.TQ[:, 128 * q:128 * q + 128], T.P4[:, 0:128], scale=T.DIF[:, q:q + 1])
+            tt("skv cl iot", "m2", T.VC[:], T.SKV[:].indirect(T.CL[:]), T.IOT[:], OP.add)
+            tt("m2 " + fo, "xc", T.XC[:], T.VC[:], F[:, 0:256], OP.max)
             ts(fo, "eq", EQ, F[:, 0:256], -2.0, OP.mult, NEG, OP.add)
         else:
-            tt("hl cc " + fo + " " + fg, "xc", T.XC[:], F[:, 0:512].indirect(T.HL[:]), T.CC[:], OP.max)
-        ts("xig", "mg", T.MG[:], T.XI[:, 0:256], B - 1, OP.bitwise_and)
+            tt("m2 wc", "xc", T.XC[:], M2, T.WC[:], OP.max)
+        ts("xig0 xig1", "mg", T.MG[:], T.XI[:, 0:256], B - 1, OP.bitwise_and)
         tt("eq mg", "t2", T2, EQ, T.MG[:], OP.min)
         tt("t2 xc", "xic", T.XI[:, 256:512], T2, T.XC[:], OP.max)
-        recs(256, "c")
+        run("gq", g.affine_select, "xig0 xig1 xic", "xf", T.XF[:], T.XI[:], [[1, 512]], OP.is_ge, 0.0, 0, 0)
+        recs(256, 256, "c")
         if t == 0:
-            th_tables()
-        mms("oneb kb", "p0", [(T.P0[:, 0], T.ONEB[0:1, 0:128], T.KB[0:1, :], True, False)])
-        cp("xig xic", "xf", T.XF[:], T.XI[:])
-        run("v", V.transpose, "xf", "xt", T.XT[:], T.XF[:])
-        for j, p in ((0, "P1"), (1, "P7")):
-            mms("xt swp", p.lower(), [(T[p][:, 0, :, u, :], T.SWP[:, 256 * u + 128 * gl:256 * u + 128 * gl + 128], T.XT[:, 8 * j:8 * j + 8, gl, :],
-                                       u + gl == 0, j == 0 and u + gl == 2) for u in range(2) for gl in range(2)])
+            later_constants()
+        mms("oneb kb", "p0", [(D, ONES, T.KB[0:1, :], True, False)])
         for j, (a, b) in enumerate(PARTS):
             tt(XRK + "rlc u%d" % j, "db%d" % j, T.DB[:, 256 * a:256 * b], T.XR[:].indirect(T.RL[:, 256 + 16 * a:256 + 16 * b]),
                T.U[:, 256 * a:256 * b], OP.subtract)
@@ -342,53 +354,54 @@ def rank_program(g, core, T, topo):
         for j, (a, b, need) in enumerate(SUMS):
             mms(need + " sq", "p0", [(T.P0[:, 0, a:b, :], T.SQ[:, 128 * q:128 * q + 128], T.AB[:, a:b, q, :], False, j == len(SUMS) - 1 and q == 15)
                                      for q in range(16)])
-        ts("xic", "flg", T.FLG[:], T.XI[:, 256:512], float(B), OP.is_ge, NEG, OP.mult)
-        tt("t2 flg", "eq", EQ, T2, T.FLG[:], OP.add)
-        tt("eq mk", "ya", T.YA[:], EQ, T.MK[:], OP.max)
+        mms("oneb npr", "p2", [(T.P2[:, 0:256], ONES, T.NPR[0:1, 0:256], True, False)])
+        act("xf", "flg", T.FLG[:], T.XF[:, 256:512], AF.Relu, bias=float(-16 * (B - 1)), scale=16.0)
+        run("v", V.transpose, "xf", "xt", T.XT[:], T.XF[:])
+        swap("P1", 0, True)
         if t:
-            save_numbers(True)
-        new_saved_clause()
-        D = T.P0[:, 0]
+            new_saved_clause()
+        tt("t2 flg", "eq", EQ, T2, T.FLG[:], OP.subtract)
+        tt("eq mk", "ya", T.YA[:], EQ, T.MK[:], OP.max)
         tt("p0 tha", "nov", T.NOV[:], D, T.THA[:], OP.is_le)
-        run("v", V.tensor_tensor_scan, "rst0 nov", "ns", T.NS[:], T.RST[:, 0:256], T.NOV[:], 0.0, OP.mult, OP.add)
-        tt("ns thr", "l8", lf(8), T.NS[:, 15::16], lf(3), OP.is_gt)
-        ts("l8", "l9", lf(9), lf(8), -2.0 * NEG, OP.mult, NEG, OP.add)
-        tt("l9 bcc diag", "ex", T.EX[:], lf(9).indirect(T.BCC[:]), T.DIAG[:], OP.mult)
-        mms("ex blkb", "p2", [(T.P2[:, 0:256], T.BLKB[:], T.EX[:], True, True)])
+        scan("rst0 nov", "ns", T.NS[:], T.RST[:, 0:256], T.NOV[:], OP.add)
         tt("p0 nov", "ky", T.KY[:], D, T.NOV[:], OP.mult)
-        run("v", V.tensor_tensor_scan, "rst0 ky", "km", T.KM[:], T.RST[:, 0:256], T.KY[:], 0.0, OP.mult, OP.max)
+        tt("ns thr", "l8", T.SB[:], T.NS[:, 15::16], lf(3), OP.is_gt)
+        mms("l8 tq", "p2", [(T.P2[:, q:256:16], T.TQ[:, 128 * q:128 * q + 128], T.SB[:], False, q == 15) for q in range(16)])
+        swap("P7", 1, False)
+        mms("oneb npr", "p3", [(T.P3[:], ONES, T.NPR[0:1, :], True, False)])
+        scan("rst0 ky", "km", T.KM[:], T.RST[:, 0:256], T.KY[:], OP.max)
         tt("ns thr", "l10", lf(10), T.NS[:, 15::16], lf(3), OP.is_le)
         tt("km bc15 ky", "mask", T.MASK[:], T.KM[:].indirect(T.BC15[:]), T.KY[:], OP.is_equal)
-        tt("l10 l0", "l11", lf(11), lf(10), lf(0), OP.mult)
+        tt("l10 sav", "l11", lf(11), lf(10), SG, OP.mult)
         tt("p1 mask", "mx0", T.MX[:, 0:256], T.P1[:, 0], T.MASK[:], OP.mult)
+        scan("rst0 mx0", "sc0", T.SC[:, 0:256], T.RST[:, 0:256], T.MX[:, 0:256], OP.add)
         if last:
             sv_payload()
-        run("v", V.tensor_tensor_scan, "rst0 mx0", "sc0", T.SC[:, 0:256], T.RST[:, 0:256], T.MX[:, 0:256], 0.0, OP.mult, OP.add)
+        tt("sc0 l8", "l12", lf(12), T.SC[:, 15:256:16], T.SB[:], OP.mult)
         tt("p2 ya", "m1", M1, T.P2[:, 0:256], T.YA[:], OP.min)
-        tt("sc0 l8", "l12", lf(12), T.SC[:, 15:256:16], lf(8), OP.mult)
-        tt("m1 base", fo, F[:, 0:256], M1, T.BASE[:], OP.max)
         tt("l12 l11", "i6", li(6), lf(12), lf(11), OP.add)
+        tt("m1 base", fo, F[:, 0:256], M1, T.BASE[:], OP.max)
         if not last:
-            ts("i6", "i7", li(7), li(6), 1023, OP.bitwise_and)
-            ts("i6", "i8", li(8), li(6), 10, OP.arith_shift_right, 2047, OP.bitwise_and)
-            ts("i7", "fl", T.FL[:], li(7), -16.0, OP.add)
+            ts("i6", "i8", li(8), li(6), 1023, OP.bitwise_and)
+            ts("i6", "i9", li(9), li(6), 10, OP.arith_shift_right, 2047, OP.bitwise_and)
+            ts("i8", "fl", T.FL[:], li(8), -16.0, OP.add)
             C = T["COL%d" % t]
-            ts("i8", "cols", C[:, 256:272], li(8), -592.0, OP.add)
+            ts("i9", "cols", C[:, 256:272], li(9), -592.0, OP.add)
             cp("fl " + fo + " " + fg, "col", C[:, 0:256], F[:, 0:512].indirect(T.FL[:]))
             d = 1 + t % (N - 1)
             dst = T.cores[(rank + d) % N]
             rel = routes(topo, core, dst)
-            before("gc", ["cols", "col"], [])
+            before("gq", ["cols", "col"], [])
             if rel:
                 w = 272 // len(rel)
                 tr = []
                 for k, c in enumerate(rel):
                     rid, pid = topo.addr(c, core)
                     es = topo.engines(core, c)
-                    tr.append(RemoteDMATransfer(dst_ids=[DstId(rid=rid, pnc=pid)], dma_engine_mask=only(es[4 * k:], 4),
+                    tr.append(RemoteDMATransfer(dst_ids=[DstId(rid=rid, pnc=pid)], dma_engine_mask=only(es[HOP * k:], HOP),
                                                 remote_sem=T.sem["in%d" % t], src=C[:, k * w:(k + 1) * w], dst=T["RB%d" % t][:, 0:w]))
                 g.remote_dma_fused(tr, local_sem=T.sem.sent)
-                sent += 4 * len(rel)
+                sent += HOP * len(rel)
             else:
                 rid, pid = topo.addr(dst, core)
                 g.remote_dma(T["F%d" % (t + 1)][:, 256:528], C[:], T.sem["arr%d" % t], T.sem.sent, pid, rid, topo.mask(core, dst))
@@ -397,76 +410,73 @@ def rank_program(g, core, T, topo):
             rin = routes(topo, src, core)
             n = sum(len(topo.engines(c, core)) for c in rin) if rin else len(topo.engines(src, core))
             arrive("arr%d" % t, n, "f%dg f%ds" % (t + 1, t + 1))
+            act(fo, "f%do" % (t + 1), T["F%d" % (t + 1)][:, 0:256], F[:, 0:256])
+            act(fo, "wn", T.WN[:], F[:, 0:256], scale=-1.0)
+            act("m1", "ya", T.YA[:], M1)
+            mms("l8 diag", "p2", [(T.P2[:, 256:272], T.DIAG[:, 0:128], T.SB[:], True, True)])
             sv_payload()
-        tt("p7 mask", "mx1", T.MX[:, 256:512], T.P7[:, 0], T.MASK[:], OP.mult)
-        run("v", V.tensor_tensor_scan, "rst1 mx1", "sc1", T.SC[:, 256:512], T.RST[:, 256:512], T.MX[:, 256:512], 0.0, OP.mult, OP.add)
         tt("l10 l4", "l13", lf(13), lf(10), lf(4), OP.mult)
-        tt("sc1 l8", "l14", lf(14), T.SC[:, 271::16], lf(8), OP.mult)
-        tt("l13 l14", "i9", li(9), lf(13), lf(14), OP.add)
-        ts("i9", "i10", li(10), li(9), 10, OP.arith_shift_right, 2047, OP.bitwise_and)
-        ts("i9", "i11", li(11), li(9), 1023, OP.bitwise_and)
-        ts("i10", "l15", lf(15), li(10), -592.0, OP.add)
-        ts("i11", "l16", lf(16), li(11), -16.0, OP.add)
+        tt("p7 mask", "mx1", T.MX[:, 256:512], T.P7[:, 0], T.MASK[:], OP.mult)
+        scan("rst1 mx1", "sc1", T.SC[:, 256:512], T.RST[:, 256:512], T.MX[:, 256:512], OP.add)
+        tt("sc1 l8", "l14", lf(14), T.SC[:, 271::16], T.SB[:], OP.mult)
+        ts("sc1", "l17", lf(17), T.SC[:, 271::16], float(2 * B), OP.is_ge)
+        tt("l13 l14", "i10", li(10), lf(13), lf(14), OP.add)
+        tt("l17 l8", "l18", lf(18), lf(17), T.SB[:], OP.mult)
+        ts("i10", "i14", li(14), li(10), 1023, OP.bitwise_and)
+        ts("i10", "i11", li(11), li(10), 10, OP.arith_shift_right, 2047, OP.bitwise_and)
+        act("l18", "s2a", T.S2[:, 0, :], lf(18))
+        act("l18", "s2b", T.S2[:, 1, :], lf(18), scale=-1.0)
+        mms("s2a s2b tq", "p3", [(T.P3[:, :, :, q], T.TQ[:, 128 * q:128 * q + 128], T.S2[:], False, q == 15) for q in range(16)])
+        if not last:
+            ts("i14", "l16", lf(16), li(14), -16.0, OP.add)
+        ts("i11", "i7", li(7), li(11), -592.0, OP.add)
         if not last:
             tt("l16 bcc diag", "eh", T.EH[:], lf(16).indirect(T.BCC[:]), T.DIAG[:], OP.mult)
-            mms("eh blkf", "p4", [(T.P4[:, 0:256], T.BLKF[:], T.EH[:], True, True)])
-            act("p4", "bh", T.BH[:], T.P4[:, 0:256])
-            act(fo, "f%do" % (t + 1), T["F%d" % (t + 1)][:, 0:256], F[:, 0:256])
-            cp("l15", "cl", T.CL[:], lf(15))
+            cp("i7", "cl", T.CL[:], li(7))
+            act("skv cl", "vc", T.VC[:], T.SKV[:].indirect(T.CL[:]))
+            mms("eh blkh oneh nih", "p4", [(T.P4[:, 0:256], T.BLKH[:], T.EH[:], True, True), (T.P4[:, 256:512], T.ONEH[:], T.NIH[:], True, False),
+                                           (T.P4[:, 256:512], T.BLKH[:], T.EH[:], False, True)])
             cp("l16", "hl", T.HL[:], lf(16))
-        ts("sc1", "l17", lf(17), T.SC[:, 271::16], float(2 * B), OP.is_ge)
-        tt("l17 l8", "l18", lf(18), lf(17), lf(8), OP.mult)
-        ts("l18", "l19", lf(19), lf(18), -2.0 * NEG, OP.mult, NEG, OP.add)
-        tt("l19 bcc diag", "ev", T.EV[:], lf(19).indirect(T.BCC[:]), T.DIAG[:], OP.mult)
-        if last:
-            mms("ev nblk", "p3", [(T.P3[:, 256:512], T.NBLK[:], T.EV[:], True, True)])
-        else:
-            mms("ev blkb nblk", "p3", [(T.P3[:, 0:256], T.BLKB[:], T.EV[:], True, True), (T.P3[:, 256:512], T.NBLK[:], T.EV[:], True, True)])
-            tt("skv cl bh", "cc", T.CC[:], T.SKV[:].indirect(T.CL[:]), T.BH[:], OP.add)
-            tt("p4 iot", "xc", T.XC[:], T.P4[:, 0:256], T.IOT[:], OP.is_equal)
-            tt("xc " + fo, "flg", T.FLG[:], T.XC[:], F[:, 0:256], OP.mult)
-            ts("flg", "eq", EQ, T.FLG[:], -2.0, OP.mult, NEG, OP.add)
-        if not last:
-            act("l8", "sb", T.SB[:], lf(8))
-            mms("sb diag", "p2", [(T.P2[:, 256:272], T.DIAG[:, 0:128], T.SB[:], True, True)])
-            act("m1", "ya", T.YA[:], M1)
-            tt("p3 ya", "m2", M2, T.P3[:, 0:256], T.YA[:], OP.min)
-            tt("p3 ya", "mk", T.MK[:], T.P3[:, 256:512], T.YA[:], OP.min)
+            act("p4", "ha", T.HA[:], T.P4[:, 256:512], AF.Abs)
+            tt("p3 ya", "m2", M2, T.P3[:, 0], T.YA[:], OP.min)
+            tt("p3 ya", "mk", T.MK[:], T.P3[:, 1], T.YA[:], OP.min)
             tt("m2 base", "base", T.BASE[:], M2, T.BASE[:], OP.max)
-    save_numbers(False)
-    F = T.F3
-    cp("f3o", "pi", T.PI[:], F[:, 0:256])
-    ts("pi", "qi", T.QI[:], T.PI[:], 1023, OP.bitwise_and)
-    ts("f3o", "m2", M2, F[:, 0:256], -606240.0, OP.add)
-    cp("m1", "ya", T.YA[:], M1)
-    tt("m2 qi", "yo", T.YO[:], M2, T.QI[:], OP.add)
-    tt("p3 ya", "m2", M2, T.P3[:, 256:512], T.YA[:], OP.min)
-    ts("m2", "p2", T.P2[:, 0:256], M2, 0.0, OP.is_ge)
+            act("ha", "p3", T.P3[:, 1], T.HA[:], AF.Identity, bias=-NEG, scale=2.0 * NEG)
+            tt("p4 vc ha", "m2", M2, T.P4[:, 0:256], T.VC[:], OP.add)
+            save_numbers(True)
+            tt("p3 wn", "eq", EQ, T.P3[:, 1], T.WN[:], OP.min)
+        else:
+            save_numbers(False)
+    act("m1", "ya", T.YA[:], M1)
+    cp("f3o", "pi", T.PI[:, 0:256], T.F3[:, 0:256])
+    ts("pi", "qi", T.QI[:, 0:256], T.PI[:, 0:256], 1023, OP.bitwise_and)
+    ts("f3o ya", "m2", M2, T.F3[:, 0:256], -606240.0, OP.add)
+    tt("m2 qi ya", "yo", T.YO[:], M2, T.QI[:, 0:256], OP.add)
+    tt("p3 ya", "m2", M2, T.P3[:, 1], T.YA[:], OP.min)
     ts("yo", "ym", T.YM[:], T.YO[:], -1.0, OP.max)
+    ts("m2", "p2", T.P2[:, 0:256], M2, 0.0, OP.is_ge)
     tt("p2 ym", "yo", T.YO[:], T.P2[:, 0:256], T.YM[:], OP.add)
     load("sync", T.yf[:], T.YO[:], "out", "yf", "yo")
 
-    def number(key, src, j):
-        ts(key, "n1", li(14), src, 10, OP.arith_shift_right, 2047, OP.bitwise_and)
-        ts(key, "n2", li(15), src, 1023, OP.bitwise_and)
-        ts("n1", "n3", lf(25), li(14), 512.0, OP.mult, float(-592 * 512 - 16), OP.add)
+    srcs = [("i6", li(6)), ("i10", li(10)), ("sav", SG)]
+    for j, (key, src) in enumerate(srcs):
+        ts(key, "n1%d" % j, T.PI[:, 256 + 16 * j:272 + 16 * j], src, 10, OP.arith_shift_right, 2047, OP.bitwise_and)
+        ts(key, "n2%d" % j, T.QI[:, 256 + 16 * j:272 + 16 * j], src, 1023, OP.bitwise_and)
+    ts("n10 n11 n12", "n3", T.MX[:, 0:48], T.PI[:, 256:304], 512.0, OP.mult, float(-592 * 512 - 16), OP.add)
+    for j in range(3):
         for k in range(2):
-            tt("n3 n2", "fld", T.FLD[:, 32 * j + 16 * k:32 * j + 16 * k + 16], lf(25), li(15), OP.add)
-    number("i6", li(6), 0)
-    number("i9", li(9), 1)
-    cp("l0", "i0", li(0), lf(0))
-    number("i0", li(0), 2)
+            tt("n3 n2%d" % j, "fld", T.FLD[:, 32 * j + 16 * k:32 * j + 16 * k + 16], T.MX[:, 16 * j:16 * j + 16], T.QI[:, 256 + 16 * j:272 + 16 * j], OP.add)
     for k in range(2):
-        cp("l1", "fld", T.FLD[:, 96 + 16 * k:112 + 16 * k], lf(1))
+        cp("sav", "fld", T.FLD[:, 96 + 16 * k:112 + 16 * k], SCL)
     run("v", V.transpose, "fld", "flt", T.FLT[:], T.FLD[:])
+    ts("flt mu0", "fo", T.FO[:], T.FLT[:, :, 0, :], T.MU0[:, 0:1], OP.mult)
+    ts("flt mu1", "fp", T.FP[:], T.FLT[:, :, 1, :], T.MU1[:, 0:1], OP.mult)
+    tt("fo fp", "fo", T.FO[:], T.FO[:], T.FP[:], OP.add)
     for j, y in enumerate((T.yg, T.yc, T.ysg, T.yk)):
-        ts("flt mu0", "fo%d" % j, T.FO[:, 16 * j:16 * j + 16], T.FLT[:, 32 * j:32 * j + 16], T.MU0[:, 0:1], OP.mult)
-        ts("flt mu1", "fp%d" % j, T.FP[:, 16 * j:16 * j + 16], T.FLT[:, 32 * j + 16:32 * j + 32], T.MU1[:, 0:1], OP.mult)
-        tt("fo%d fp%d" % (j, j), "fq%d" % j, T.FO[:, 16 * j:16 * j + 16], T.FO[:, 16 * j:16 * j + 16], T.FP[:, 16 * j:16 * j + 16], OP.add)
-        load("sync", y[:], T.FO[:, 16 * j:16 * j + 16], "out", "y%d" % j, "fq%d" % j)
+        load("sync" if j % 2 else "s", y[:], T.FO[:, j, :], "out", "y%d" % j, "fo")
     g.sync.wait_ge(T.sem.out, cnt["out"])
     g.wait_ge(T.sem.sent, sent)
-    for q in ("v", "s", "pe", "gc"):
+    for q in ("v", "s", "pe", "gq"):
         g.sync.wait_ge(T.sem[q], cnt[q])
     for s in LOADS:
         if not any(k[1] == s for k in seen):

@@ -8,6 +8,7 @@ B = 1 << 21
 KE = 592 * 1024 + 16
 PARTS = [(0, 4), (4, 8), (8, 12), (12, 14), (14, 16)]
 SUMS = [(0, 4, "ab0"), (4, 8, "ab1"), (8, 12, "ab2"), (12, 16, "ab3 ab4")]
+LAT, GAP, PATIENCE = 0.09, 0.5, 0.7
 HOP = 8
 LOADS = ["l_gs0", "l_gs1", "l_gf0", "l_gf1", "l_gc0", "l_gc1", "l_gfr", "l_fr", "l_sk", "l_th", "l_x0", "l_x1"]
 
@@ -67,6 +68,71 @@ def only(engines, n):
     return sum(1 << e for e in engines[:n])
 
 
+def hand(ins):
+    return None
+
+
+SMALL = "sl fl cl hl thr sav cols pm mui mu0 mu1 lik bc15 bcc tl ta tb s2a s2b fo fp npr thf oneh dif fld".split()
+LONG = {"cg": .37, "mask": .37, "eh": .37, "col": .37, "wc": .39, "vc": .39, "xt": .44, "skv": .44, "zic": .44, "zig0": .23, "zig1": .23,
+        "xf": 1.05, "ns": .13, "sku0": .44, "sku1": .44, "tq": .13, "sq": .1, "idf": .4, "r8": .4, "r16": .6, "c16": .16, "pio": .16,
+        "iot": .55, "kb": .55, "bia": .55, "sw0": .3, "sw1": .3, "sw2": .3, "sw3": .3}
+
+
+def guess(q, key):
+    if key in LONG:
+        return LONG[key]
+    if key in SMALL or key[0] in "li" and key[1:].isdigit():
+        return 0.075
+    if key[0] == "u" and key[1:].isdigit() or key[:2] == "db" and key[2:].isdigit():
+        a, b = PARTS[int(key[-1])]
+        return 0.06 + 0.32 * (b - a)
+    if key[:2] == "ab":
+        a, b = PARTS[int(key[-1])]
+        return 0.02 + 0.213 * (b - a)
+    return 0.13 if key[-2:] in ("g0", "g1") else 0.235
+
+
+def plan(nodes):
+    m = len(nodes)
+    succ = [[] for _ in range(m)]
+    left = [len(x["deps"]) for x in nodes]
+    for n, x in enumerate(nodes):
+        for d in x["deps"]:
+            succ[d].append(n)
+    way = [0.0] * m
+    for n in range(m - 1, -1, -1):
+        way[n] = nodes[n]["cost"] + nodes[n]["lat"] + max([way[k] for k in succ[n]] + [0.0])
+    start = [0.0] * m
+    free, can, order = {}, {}, []
+    for n in range(m):
+        if not left[n]:
+            can.setdefault(nodes[n]["q"], []).append(n)
+    while len(order) < m:
+        best = None
+        for q in can:
+            if can[q]:
+                t = max(free.get(q, 0.0), min(start[n] for n in can[q]))
+                if best is None or t < best[0]:
+                    best = (t, q)
+        t, q = best
+        now = [n for n in can[q] if start[n] <= t + 1e-9]
+        n = max(now, key=lambda k: (way[k], -k))
+        for k in sorted(can[q], key=lambda k: -way[k]):
+            if way[k] > way[n] + GAP and start[k] < t + PATIENCE * nodes[n]["cost"]:
+                n = k
+                break
+        t = max(t, start[n])
+        can[q].remove(n)
+        order.append((t, len(order), n))
+        free[q] = t + nodes[n]["cost"]
+        for k in succ[n]:
+            left[k] -= 1
+            start[k] = max(start[k], t + nodes[n]["cost"] + nodes[n]["lat"])
+            if not left[k]:
+                can.setdefault(nodes[k]["q"], []).append(k)
+    return [n for _, _, n in sorted(order)]
+
+
 def relay(g, core, T, topo):
     sent = 0
     for t in range(RO - 1):
@@ -94,46 +160,47 @@ def rank_program(g, core, T, topo):
         return relay(g, core, T, topo)
     ENG = {"v": g.vector, "s": g.scalar, "pe": g.tensor, "gq": g, "sync": g.sync}
     V = g.vector
-    cnt, seen, wr, rd = {}, {}, {}, {}
+    nodes, lastw, readers = [], {}, {}
 
-    def before(q, reads, writes):
-        need = {}
-        for k in reads:
-            for tok in wr.get(k, []):
-                need[tok[1]] = max(need.get(tok[1], 0), tok[2])
+    def add(q, emit, reads, writes, cost, lat, sem, inc):
+        reads, writes = reads.split(), writes.split()
+        deps = set(lastw[k] for k in reads + writes if k in lastw)
         for k in writes:
-            for tok in wr.get(k, []) + rd.get(k, []):
-                if tok[0] != q or q != "pe":
-                    need[tok[1]] = max(need.get(tok[1], 0), tok[2])
-        for s in sorted(need):
-            if seen.get((q, s), 0) < need[s]:
-                ENG[q].wait_ge(T.sem[s], need[s])
-                seen[(q, s)] = need[s]
-
-    def after(q, ins, sem, n, reads, writes):
-        cnt[sem] = cnt.get(sem, 0) + n
-        ins.then_inc(T.sem[sem], n)
-        tok = (q, sem, cnt[sem])
+            deps |= readers.get(k, set())
+        n = len(nodes)
+        nodes.append({"q": q, "emit": emit, "deps": deps, "cost": cost, "lat": lat, "sem": sem, "inc": inc})
         for k in writes:
-            wr[k] = [tok]
-            rd[k] = []
+            lastw[k] = n
+            readers[k] = set()
         for k in reads:
-            rd.setdefault(k, []).append(tok)
+            readers.setdefault(k, set()).add(n)
 
     def run(q, fn, reads, writes, *a, **kw):
-        reads, writes = reads.split(), writes.split()
-        before(q, reads, writes)
-        after(q, fn(*a, **kw), q, 1, reads, writes)
+        add(q, lambda: fn(*a, **kw), reads, writes, guess(q, writes.split()[0]), LAT, q, 1)
 
     def load(q, out, in_, sem, key, reads=""):
-        reads = reads.split()
-        before(q, reads, [key])
-        after("dma_" + sem, ENG[q].dma_start(out, in_), sem, 16, reads, [key])
+        add(q, lambda: ENG[q].dma_start(out, in_), reads, key, 0.06, 1.9, sem, 16)
 
-    def arrive(sem, n, keys):
-        for k in keys.split():
-            wr[k] = [("net", sem, n)]
-            rd[k] = []
+    def issue():
+        cnt, seen, tok = {}, {}, {}
+        for n in plan(nodes):
+            x = nodes[n]
+            q = x["q"]
+            need = {}
+            for d in x["deps"]:
+                if d in tok and not (q == "pe" and tok[d][0] == "pe"):
+                    need[tok[d][0]] = max(need.get(tok[d][0], 0), tok[d][1])
+            for sm in sorted(need):
+                if q in ENG and seen.get((q, sm), 0) < need[sm]:
+                    ENG[q].wait_ge(T.sem[sm], need[sm])
+                    seen[(q, sm)] = need[sm]
+            ins = x["emit"]()
+            if x["sem"]:
+                cnt[x["sem"]] = cnt.get(x["sem"], 0) + x["inc"]
+                tok[n] = (x["sem"], cnt[x["sem"]])
+                if ins is not None:
+                    ins.then_inc(T.sem[x["sem"]], x["inc"])
+        return cnt, seen
 
     def tt(reads, w, out, a, b, op):
         run("v", V.tensor_tensor, reads, w, out, a, b, op)
@@ -154,11 +221,11 @@ def rank_program(g, core, T, topo):
         run("s", g.scalar.activation, reads, w, out, a, func, **kw)
 
     def mms(reads, w, calls):
-        reads, w = reads.split(), w.split()
-        before("pe", reads, w)
-        for c in calls:
-            ins = g.tensor.matmul(*c)
-        after("pe", ins, "pe", 1, reads, w)
+        def emit():
+            for c in calls:
+                ins = g.tensor.matmul(*c)
+            return ins
+        add("pe", emit, reads, w, 0.9 if len(calls) == 16 else 1.7 if len(calls) == 4 else 0.25 * len(calls), LAT, "pe", 1)
 
     def lf(j, n=1):
         return T.LF[:, 16 * j:16 * j + 16 * n]
@@ -225,20 +292,21 @@ def rank_program(g, core, T, topo):
     cp("gfr", "gfb", T.GFB[:], T.GFR[:])
     mms("r8 gfb", "p2", [(T.P2[:, 0:256], T.R8[:], T.GFB[:], True, True)])
     act("p2", "bg", T.BG[:], T.P2[:, 0:256])
-    ts("fri", "p6", T.P6[:, 0:256], T.FRI[:], 2.0, OP.mult, float(KE), OP.add)
-    ts("fri", "p5", T.P5[:, 0:256], T.FRI[:], 0.0, OP.is_lt, NEG, OP.mult)
-    tt("p6 frq", "ow", T.OW[:], T.P6[:, 0:256], T.FRQ[:], OP.subtract)
+    ts("fri", "m1", T.P6[:, 0:256], T.FRI[:], 2.0, OP.mult, float(KE), OP.add)
+    ts("fri", "eq", T.P5[:, 0:256], T.FRI[:], 0.0, OP.is_lt, NEG, OP.mult)
+    tt("m1 frq", "ow", T.OW[:], T.P6[:, 0:256], T.FRQ[:], OP.subtract)
     cp("tl", "sl", T.SL[:], T.TL[:, 0, :])
-    tt("p5 ow", "f0o", T.F0[:, 0:256], T.P5[:, 0:256], T.OW[:], OP.add)
+    tt("eq ow", "f0o", T.F0[:, 0:256], T.P5[:, 0:256], T.OW[:], OP.add)
     cp("tl", "fl", T.FL[:], T.TL[:, 1, :])
     act("f0o", "f0g", T.F0[:, 256:512], T.F0[:, 0:256])
+    BANK = {"P5": "eq t2", "P6": "m1 m2"}
     for j, p in ((0, "P5"), (1, "P6")):
         cs = slice(512 * j, 512 * j + 512)
-        ts("ski", p.lower(), T[p][:], T.SKI[:, cs], 1024.0, OP.is_ge, float(-(1 << 20) - 2 * B), OP.mult)
+        ts("ski", BANK[p], T[p][:], T.SKI[:, cs], 1024.0, OP.is_ge, float(-(1 << 20) - 2 * B), OP.mult)
         ts("ski", "sku%d" % j, T.SKU[:, cs], T.SKI[:, cs], 1024.0, OP.mult, float(KE + B), OP.add)
     for j, p in ((0, "P5"), (1, "P6")):
         cs = slice(512 * j, 512 * j + 512)
-        tt("%s sku%d" % (p.lower(), j), "skv", T.SKV[:, cs], T[p][:], T.SKU[:, cs], OP.add)
+        tt("%s sku%d" % (BANK[p], j), "skv", T.SKV[:, cs], T[p][:], T.SKU[:, cs], OP.add)
     cp("tl", "cl", T.CL[:], T.TL[:, 2, :])
     act("p0", "diag", T.DIAG[:], T.P0[:, 0])
     act("p4", "blkf", T.BLKF[:], T.P4[:, 0:128])
@@ -334,8 +402,8 @@ def rank_program(g, core, T, topo):
         if t == 0:
             for q in range(16):
                 act("p4 dif", "tq", T.TQ[:, 128 * q:128 * q + 128], T.P4[:, 0:128], scale=T.DIF[:, q:q + 1])
-            tt("skv cl iot", "m2", T.VC[:], T.SKV[:].indirect(T.CL[:]), T.IOT[:], OP.add)
-            tt("m2 " + fo, "xc", T.XC[:], T.VC[:], F[:, 0:256], OP.max)
+            tt("skv cl iot", "vc", T.VC[:], T.SKV[:].indirect(T.CL[:]), T.IOT[:], OP.add)
+            tt("vc " + fo, "xc", T.XC[:], T.VC[:], F[:, 0:256], OP.max)
             ts(fo, "eq", EQ, F[:, 0:256], -2.0, OP.mult, NEG, OP.add)
         else:
             tt("m2 wc", "xc", T.XC[:], M2, T.WC[:], OP.max)
@@ -391,28 +459,28 @@ def rank_program(g, core, T, topo):
             d = 1 + t % (N - 1)
             dst = T.cores[(rank + d) % N]
             rel = routes(topo, core, dst)
-            before("gq", ["cols", "col"], [])
+            tr = []
             if rel:
                 w = 272 // len(rel)
-                tr = []
                 for k, c in enumerate(rel):
                     rid, pid = topo.addr(c, core)
                     es = topo.engines(core, c)
                     tr.append(RemoteDMATransfer(dst_ids=[DstId(rid=rid, pnc=pid)], dma_engine_mask=only(es[HOP * k:], HOP),
                                                 remote_sem=T.sem["in%d" % t], src=C[:, k * w:(k + 1) * w], dst=T["RB%d" % t][:, 0:w]))
-                g.remote_dma_fused(tr, local_sem=T.sem.sent)
+                add("gq", lambda tr=tr: hand(g.remote_dma_fused(tr, local_sem=T.sem.sent)), "cols col", "go", 1.0, 5.0, None, 0)
                 sent += HOP * len(rel)
             else:
                 rid, pid = topo.addr(dst, core)
-                g.remote_dma(T["F%d" % (t + 1)][:, 256:528], C[:], T.sem["arr%d" % t], T.sem.sent, pid, rid, topo.mask(core, dst))
+                add("gq", lambda a=(T["F%d" % (t + 1)][:, 256:528], C[:], T.sem["arr%d" % t], T.sem.sent, pid, rid, topo.mask(core, dst)):
+                    hand(g.remote_dma(*a)), "cols col", "go", 1.0, 3.0, None, 0)
                 sent += len(topo.engines(core, dst))
             src = T.cores[(rank - d) % N]
             rin = routes(topo, src, core)
             n = sum(len(topo.engines(c, core)) for c in rin) if rin else len(topo.engines(src, core))
-            arrive("arr%d" % t, n, "f%dg f%ds" % (t + 1, t + 1))
+            add("net", lambda: None, "go", "f%dg f%ds" % (t + 1, t + 1), 0.0, 0.0, "arr%d" % t, n)
             act(fo, "f%do" % (t + 1), T["F%d" % (t + 1)][:, 0:256], F[:, 0:256])
             act(fo, "wn", T.WN[:], F[:, 0:256], scale=-1.0)
-            act("m1", "ya", T.YA[:], M1)
+            act("m1 m2 " + fo, "ya", T.YA[:], M1)
             mms("l8 diag", "p2", [(T.P2[:, 256:272], T.DIAG[:, 0:128], T.SB[:], True, True)])
             sv_payload()
         tt("l10 l4", "l13", lf(13), lf(10), lf(4), OP.mult)
@@ -447,11 +515,11 @@ def rank_program(g, core, T, topo):
             tt("p3 wn", "eq", EQ, T.P3[:, 1], T.WN[:], OP.min)
         else:
             save_numbers(False)
-    act("m1", "ya", T.YA[:], M1)
-    cp("f3o", "pi", T.PI[:, 0:256], T.F3[:, 0:256])
-    ts("pi", "qi", T.QI[:, 0:256], T.PI[:, 0:256], 1023, OP.bitwise_and)
+    act("m1 m2 f3o", "ya", T.YA[:], M1)
+    cp("f3o", "pig0 pig1", T.PI[:, 0:256], T.F3[:, 0:256])
+    ts("pig0 pig1", "qig0 qig1", T.QI[:, 0:256], T.PI[:, 0:256], 1023, OP.bitwise_and)
     ts("f3o ya", "m2", M2, T.F3[:, 0:256], -606240.0, OP.add)
-    tt("m2 qi ya", "yo", T.YO[:], M2, T.QI[:, 0:256], OP.add)
+    tt("m2 qig0 qig1 ya", "yo", T.YO[:], M2, T.QI[:, 0:256], OP.add)
     tt("p3 ya", "m2", M2, T.P3[:, 1], T.YA[:], OP.min)
     ts("yo", "ym", T.YM[:], T.YO[:], -1.0, OP.max)
     ts("m2", "p2", T.P2[:, 0:256], M2, 0.0, OP.is_ge)
@@ -460,12 +528,12 @@ def rank_program(g, core, T, topo):
 
     srcs = [("i6", li(6)), ("i10", li(10)), ("sav", SG)]
     for j, (key, src) in enumerate(srcs):
-        ts(key, "n1%d" % j, T.PI[:, 256 + 16 * j:272 + 16 * j], src, 10, OP.arith_shift_right, 2047, OP.bitwise_and)
-        ts(key, "n2%d" % j, T.QI[:, 256 + 16 * j:272 + 16 * j], src, 1023, OP.bitwise_and)
-    ts("n10 n11 n12", "n3", T.MX[:, 0:48], T.PI[:, 256:304], 512.0, OP.mult, float(-592 * 512 - 16), OP.add)
+        ts(key, "pic", T.PI[:, 256 + 16 * j:272 + 16 * j], src, 10, OP.arith_shift_right, 2047, OP.bitwise_and)
+        ts(key, "qic", T.QI[:, 256 + 16 * j:272 + 16 * j], src, 1023, OP.bitwise_and)
+    ts("pic", "mx0", T.MX[:, 0:48], T.PI[:, 256:304], 512.0, OP.mult, float(-592 * 512 - 16), OP.add)
     for j in range(3):
         for k in range(2):
-            tt("n3 n2%d" % j, "fld", T.FLD[:, 32 * j + 16 * k:32 * j + 16 * k + 16], T.MX[:, 16 * j:16 * j + 16], T.QI[:, 256 + 16 * j:272 + 16 * j], OP.add)
+            tt("mx0 qic", "fld", T.FLD[:, 32 * j + 16 * k:32 * j + 16 * k + 16], T.MX[:, 16 * j:16 * j + 16], T.QI[:, 256 + 16 * j:272 + 16 * j], OP.add)
     for k in range(2):
         cp("sav", "fld", T.FLD[:, 96 + 16 * k:112 + 16 * k], SCL)
     run("v", V.transpose, "fld", "flt", T.FLT[:], T.FLD[:])
@@ -474,10 +542,11 @@ def rank_program(g, core, T, topo):
     tt("fo fp", "fo", T.FO[:], T.FO[:], T.FP[:], OP.add)
     for j, y in enumerate((T.yg, T.yc, T.ysg, T.yk)):
         load("sync" if j % 2 else "s", y[:], T.FO[:, j, :], "out", "y%d" % j, "fo")
+    cnt, seen = issue()
     g.sync.wait_ge(T.sem.out, cnt["out"])
     g.wait_ge(T.sem.sent, sent)
     for q in ("v", "s", "pe", "gq"):
         g.sync.wait_ge(T.sem[q], cnt[q])
-    for s in LOADS:
-        if not any(k[1] == s for k in seen):
-            g.sync.wait_ge(T.sem[s], 16)
+    for sm in LOADS:
+        if not any(k[1] == sm for k in seen):
+            g.sync.wait_ge(T.sem[sm], 16)

@@ -8,7 +8,8 @@ B = 1 << 21
 KE = 592 * 1024 + 16
 PARTS = [(0, 4), (4, 8), (8, 12), (12, 14), (14, 16)]
 SUMS = [(0, 4, "ab0"), (4, 8, "ab1"), (8, 12, "ab2"), (12, 16, "ab3 ab4")]
-LAT, GAP, PATIENCE = 0.09, 0.5, 0.7
+HELP = [[], [4], [4], []]
+LAT, GAP, PATIENCE = 0.14, 0.8, 0.3
 HOP = 8
 LOADS = ["l_gs0", "l_gs1", "l_gf0", "l_gf1", "l_gc0", "l_gc1", "l_gfr", "l_fr", "l_sk", "l_th", "l_x0", "l_x1"]
 
@@ -49,7 +50,7 @@ SCRATCH = {
     "NOV": b16(256), "NS": b16(256), "SV": b16(256), "SB": b16(16), "S2": b16(2, 16), "KY": f32(256), "KM": f32(256), "MASK": b16(256),
     "MX": f32(512), "SC": f32(512), "EH": ("sbuf", [128, 256], "float16"), "HA": f32(256), "WN": f32(256),
     "LF": f32(512), "LI": i32(256), "SAV": i32(32),
-    "FLD": f32(128), "FLT": f32(4, 2, 16), "FO": f32(4, 16), "FP": f32(4, 16), "YO": f32(256), "YM": f32(256),
+    "FLD": f32(4, 2, 16), "FLT": f32(4, 2, 16), "FO": f32(4, 16), "FP": f32(4, 16), "YO": f32(256), "YM": f32(256),
     "P0": ("psum", [128, 2, 16, 16], "float32"), "P1": ("psum", [128, 2, 8, 2, 16], "float32"), "P2": ("psum", [128, 512], "float32"),
     "P3": ("psum", [128, 2, 16, 16], "float32"), "P4": ("psum", [128, 512], "float32"), "P5": ("psum", [128, 512], "float32"),
     "P6": ("psum", [128, 512], "float32"), "P7": ("psum", [128, 2, 8, 2, 16], "float32"),
@@ -72,9 +73,9 @@ def hand(ins):
     return None
 
 
-SMALL = "sl fl cl hl thr sav cols pm mui mu0 mu1 lik bc15 bcc tl ta tb s2a s2b fo fp npr thf oneh dif fld".split()
+SMALL = "sl fl cl hl thr sav cols pm mui mu0 mu1 lik bc15 bcc tl ta tb s2a s2b fo fp npr thf oneh dif fld0 fld1 fle0 fle1".split()
 LONG = {"cg": .37, "mask": .37, "eh": .37, "col": .37, "wc": .39, "vc": .39, "xt": .44, "skv": .44, "zic": .44, "zig0": .23, "zig1": .23,
-        "xf": 1.05, "ns": .13, "sku0": .44, "sku1": .44, "tq": .13, "sq": .1, "idf": .4, "r8": .4, "r16": .6, "c16": .16, "pio": .16,
+        "xf": 1.05, "skf": 1.9, "ns": .13, "sku0": .44, "sku1": .44, "tq": .13, "sq": .1, "idf": .4, "r8": .4, "r16": .6, "c16": .16, "pio": .16,
         "iot": .55, "kb": .55, "bia": .55, "sw0": .3, "sw1": .3, "sw2": .3, "sw3": .3}
 
 
@@ -277,9 +278,9 @@ def rank_program(g, core, T, topo):
     mms("r8", "p4", [(T.P4[:, 0:128], T.R8[:], T.R8[:], True, True)])
     mms("r16", "p0", [(T.P0[:, 0], T.R16[:, 0:128], T.R16[:], True, True)])
     for j in range(8):
-        act("iot", "sq", T.SQ[:, 256 * j:256 * j + 256], T.IOT[:], scale=0.0)
+        act("oneb", "sq", T.SQ[:, 256 * j:256 * j + 256], T.ONEB[:], scale=0.0)
     for j in range(2):
-        act("iot", "swp", T.SWP[:, 2 * j:2 * j + 2], T.IOT[:], scale=0.0)
+        act("oneb", "swp", T.SWP[:, 2 * j:2 * j + 2], T.ONEB[:], scale=0.0)
     for u in range(2):
         for gl in range(2):
             sel(T.SWP[:, 2 * u + gl, :, gl, :], T.ONEF[:, :, 0, :], [[-32, 4], [-1, 16]], -16 * u, "onef swp", "sw%d" % (2 * u + gl))
@@ -299,11 +300,12 @@ def rank_program(g, core, T, topo):
     tt("eq ow", "f0o", T.F0[:, 0:256], T.P5[:, 0:256], T.OW[:], OP.add)
     cp("tl", "fl", T.FL[:], T.TL[:, 1, :])
     act("f0o", "f0g", T.F0[:, 256:512], T.F0[:, 0:256])
+    run("gq", g.affine_select, "ski", "skf", T.SKU[:], T.SKI[:], [[1, 1024]], OP.is_ge, 0.0, 0, 0)
     BANK = {"P5": "eq t2", "P6": "m1 m2"}
     for j, p in ((0, "P5"), (1, "P6")):
         cs = slice(512 * j, 512 * j + 512)
         ts("ski", BANK[p], T[p][:], T.SKI[:, cs], 1024.0, OP.is_ge, float(-(1 << 20) - 2 * B), OP.mult)
-        ts("ski", "sku%d" % j, T.SKU[:, cs], T.SKI[:, cs], 1024.0, OP.mult, float(KE + B), OP.add)
+        act("skf", "sku%d" % j, T.SKU[:, cs], T.SKU[:, cs], AF.Identity, bias=float(KE + B), scale=1024.0)
     for j, p in ((0, "P5"), (1, "P6")):
         cs = slice(512 * j, 512 * j + 512)
         tt("%s sku%d" % (BANK[p], j), "skv", T.SKV[:, cs], T[p][:], T.SKU[:, cs], OP.add)
@@ -320,10 +322,10 @@ def rank_program(g, core, T, topo):
         cp("thi", "thf", T.THF[:], T.THI[:])
         ts("diag thf", "thd", T.THD[:], T.DIAG[:], T.THF[:, 0:1], OP.mult)
         mms("blkf thd", "p2", [(T.P2[:, 0:256], T.BLKF[:], T.THD[:], True, True)])
-        ts("kb", "rst0", T.RST[:, 0:256], T.KB[:], 15.0, OP.is_lt)
-        ts("kb", "rst1", T.RST[:, 256:512], T.KB[:], 15.0, OP.is_lt)
+        act("kb", "rst0", T.RST[:, 0:256], T.KB[:], AF.Sign, scale=-1.0, bias=15.0)
+        act("kb", "rst1", T.RST[:, 256:512], T.KB[:], AF.Sign, scale=-1.0, bias=15.0)
         run("v", V.memset, "", "thr", lf(3), 8.0)
-        run("v", V.memset, "", "mk", T.MK[:], NEG)
+        act("oneb", "mk", T.MK[:], T.ONEB[:], AF.Identity, scale=0.0, bias=NEG)
         ts("tl", "l2", lf(2), T.TL[:, 0, :], 1024.0, OP.mult, float(KE), OP.add)
         run("v", V.memset, "", "npr", T.NPR[:, 0:256], NEG)
         run("v", V.memset, "", "npr", T.NPR[:, 256:512], -NEG)
@@ -398,7 +400,8 @@ def rank_program(g, core, T, topo):
                 tt("cg p3", "xig%d" % k, T.XI[:, c], T.P3[:, 0, 8 * k:8 * k + 8, :], T.CG[:, c], OP.max)
             recs(128 * k, 128, "g%d" % k)
         for j, (a, b) in enumerate(PARTS):
-            act(XRK + "rlg%d" % (a // 8), "u%d" % j, T.U[:, 256 * a:256 * b], T.XR[:].indirect(T.RL[:, 16 * a:16 * b]))
+            if j not in HELP[t]:
+                act(XRK + "rlg%d" % (a // 8), "u%d" % j, T.U[:, 256 * a:256 * b], T.XR[:].indirect(T.RL[:, 16 * a:16 * b]))
         if t == 0:
             for q in range(16):
                 act("p4 dif", "tq", T.TQ[:, 128 * q:128 * q + 128], T.P4[:, 0:128], scale=T.DIF[:, q:q + 1])
@@ -416,6 +419,8 @@ def rank_program(g, core, T, topo):
             later_constants()
         mms("oneb kb", "p0", [(D, ONES, T.KB[0:1, :], True, False)])
         for j, (a, b) in enumerate(PARTS):
+            if j in HELP[t]:
+                cp(XRK + "rlg1 db1", "u%d" % j, T.U[:, 256 * a:256 * b], T.XR[:].indirect(T.RL[:, 16 * a:16 * b]))
             tt(XRK + "rlc u%d" % j, "db%d" % j, T.DB[:, 256 * a:256 * b], T.XR[:].indirect(T.RL[:, 256 + 16 * a:256 + 16 * b]),
                T.U[:, 256 * a:256 * b], OP.subtract)
             act("db%d" % j, "ab%d" % j, T.AB[:, a:b], T.DB[:, 256 * a:256 * b], AF.Abs)
@@ -531,12 +536,10 @@ def rank_program(g, core, T, topo):
         ts(key, "pic", T.PI[:, 256 + 16 * j:272 + 16 * j], src, 10, OP.arith_shift_right, 2047, OP.bitwise_and)
         ts(key, "qic", T.QI[:, 256 + 16 * j:272 + 16 * j], src, 1023, OP.bitwise_and)
     ts("pic", "mx0", T.MX[:, 0:48], T.PI[:, 256:304], 512.0, OP.mult, float(-592 * 512 - 16), OP.add)
-    for j in range(3):
-        for k in range(2):
-            tt("mx0 qic", "fld", T.FLD[:, 32 * j + 16 * k:32 * j + 16 * k + 16], T.MX[:, 16 * j:16 * j + 16], T.QI[:, 256 + 16 * j:272 + 16 * j], OP.add)
     for k in range(2):
-        cp("sav", "fld", T.FLD[:, 96 + 16 * k:112 + 16 * k], SCL)
-    run("v", V.transpose, "fld", "flt", T.FLT[:], T.FLD[:])
+        tt("mx0 qic", "fld%d" % k, T.FLD[:, 0:3, k, :], T.MX[:, 0:48], T.QI[:, 256:304], OP.add)
+        cp("sav", "fle%d" % k, T.FLD[:, 3, k, :], SCL)
+    run("v", V.transpose, "fld0 fld1 fle0 fle1", "flt", T.FLT[:], T.FLD[:])
     ts("flt mu0", "fo", T.FO[:], T.FLT[:, :, 0, :], T.MU0[:, 0:1], OP.mult)
     ts("flt mu1", "fp", T.FP[:], T.FLT[:, :, 1, :], T.MU1[:, 0:1], OP.mult)
     tt("fo fp", "fo", T.FO[:], T.FO[:], T.FP[:], OP.add)

from concourse.bass import DstId, RemoteDMATransfer
from concourse.mybir import AluOpType as OP, ActivationFunctionType as AF

N = 8
RO = 4
NEG = -8388608.0
B = 1 << 21
KE = 592 * 1024 + 16
PARTS = [(0, 4), (4, 8), (8, 12), (12, 14), (14, 16)]
SUMS = [(0, 4, "ab0"), (4, 8, "ab1"), (8, 12, "ab2"), (12, 16, "ab3 ab4")]
HELP = [[], [4], [4], []]
LAT, GAP, PATIENCE = 0.14, 0.8, 0.3
HOP = 8
LOADS = ["l_gs0", "l_gs1", "l_gf0", "l_gf1", "l_gc0", "l_gc1", "l_gfr", "l_fr", "l_sk", "l_th", "l_x0", "l_x1"]


def f32(*s):
    return ("sbuf", [128] + list(s), "float32")


def i32(*s):
    return ("sbuf", [128] + list(s), "int32")


def b16(*s):
    return ("sbuf", [128] + list(s), "bfloat16")


def u16(*s):
    return ("sbuf", [128] + list(s), "uint16")


SCRATCH = {
    "XR": b16(4096), "SKI": i32(1024), "SKU": f32(1024), "SKV": f32(1024), "FRI": i32(256), "FRQ": i32(256), "OW": f32(256),
    "BASE": f32(256), "MK": f32(256), "YA": f32(256), "FLG": f32(256), "F0": f32(528), "F1": f32(528), "F2": f32(528), "F3": f32(528),
    "COL0": f32(272), "COL1": f32(272), "COL2": f32(272), "RB0": f32(136), "RB2": f32(136),
    "TT": i32(96), "TX": i32(3, 2, 16), "TA": f32(3, 16), "TB": f32(3, 16), "TL": f32(3, 16),
    "GFR": ("sbuf", [8, 256], "int32"), "GFB": ("sbuf", [8, 256], "bfloat16"), "R16": ("sbuf", [16, 256], "bfloat16"), "R8": ("sbuf", [8, 128], "bfloat16"),
    "THI": i32(1), "THF": f32(1), "THD": f32(256), "THA": f32(256), "THB": f32(256), "THW": i32(256),
    "ONEB": b16(256), "ONEF": f32(4, 2, 16), "ONEG": f32(128), "IDF": f32(128), "IDB": b16(128),
    "BLKF": f32(128), "BLKH": ("sbuf", [128, 128], "float16"), "NPR": ("sbuf", [1, 512], "bfloat16"),
    "ONEH": ("sbuf", [1, 128], "float16"), "NIH": ("sbuf", [1, 256], "float16"),
    "DIAG": b16(256), "DIF": f32(16), "SQ": b16(2048), "TQ": b16(2048), "SWP": f32(4, 4, 2, 16),
    "KB": b16(256), "RST": b16(512), "IOT": f32(256), "BIA": f32(256), "BG": f32(256),
    "C16": f32(16), "PIO": i32(16), "PM": i32(16), "LIK": f32(16), "MUI": i32(16), "MU1": f32(16), "MU0": f32(16),
    "BC15": u16(16), "SL": u16(16), "FL": u16(16), "CL": u16(16), "HL": u16(16), "BCC": u16(16),
    "CG": f32(256), "VC": f32(256), "WC": f32(256), "XC": f32(256), "MG": i32(256),
    "XI": i32(512), "PI": i32(512), "QI": i32(512), "ZI": i32(512), "RI": i32(512), "RL": u16(512),
    "U": b16(4096), "DB": b16(4096), "AB": b16(16, 16, 16), "XF": f32(512), "XT": f32(16, 2, 16),
    "NOV": b16(256), "NS": b16(256), "SV": b16(256), "SB": b16(16), "S2": b16(2, 16), "KY": f32(256), "KM": f32(256), "MASK": b16(256),
    "MX": f32(512), "SC": f32(512), "EH": ("sbuf", [128, 256], "float16"), "HA": f32(256), "WN": f32(256),
    "LF": f32(512), "LI": i32(256), "SAV": i32(32),
    "FLD": f32(4, 2, 16), "FLT": f32(4, 2, 16), "FO": f32(4, 16), "FP": f32(4, 16), "YO": f32(256), "YM": f32(256),
    "P0": ("psum", [128, 2, 16, 16], "float32"), "P1": ("psum", [128, 2, 8, 2, 16], "float32"), "P2": ("psum", [128, 512], "float32"),
    "P3": ("psum", [128, 2, 16, 16], "float32"), "P4": ("psum", [128, 512], "float32"), "P5": ("psum", [128, 512], "float32"),
    "P6": ("psum", [128, 512], "float32"), "P7": ("psum", [128, 2, 8, 2, 16], "float32"),
}
SEMAPHORES = LOADS + ["v", "s", "pe", "gq", "out", "sent", "in0", "in2", "arr0", "arr1", "arr2"]


def routes(topo, a, b):
    if topo.may_write(a, b):
        return []
    own = [c for c in topo.cores_of(a) if c != a and topo.may_write(c, b)]
    return [[c for c in own if topo.die(c) == die][0] for die in sorted(set(topo.die(c) for c in own))]


def only(engines, n):
    return sum(1 << e for e in engines[:n])


def hand(ins):
    return None


SMALL = "sl fl cl hl thr sav cols pm mui mu0 mu1 lik bc15 bcc tl ta tb s2a s2b fo fp npr thf oneh dif fld0 fld1 fle0 fle1".split()
LONG = {"cg": .37, "mask": .37, "eh": .37, "col": .37, "wc": .39, "vc": .39, "xt": .44, "skv": .44, "zic": .44, "zig0": .23, "zig1": .23,
        "xf": 1.05, "skf": 1.9, "ns": .13, "sku0": .44, "sku1": .44, "tq": .13, "sq": .1, "idf": .4, "r8": .4, "r16": .6, "c16": .16, "pio": .16,
        "iot": .55, "kb": .55, "bia": .55, "sw0": .3, "sw1": .3, "sw2": .3, "sw3": .3}


def guess(q, key):
    if key in LONG:
        return LONG[key]
    if key in SMALL or key[0] in "li" and key[1:].isdigit():
        return 0.075
    if key[0] == "u" and key[1:].isdigit() or key[:2] == "db" and key[2:].isdigit():
        a, b = PARTS[int(key[-1])]
        return 0.06 + 0.32 * (b - a)
    if key[:2] == "ab":
        a, b = PARTS[int(key[-1])]
        return 0.02 + 0.213 * (b - a)
    return 0.13 if key[-2:] in ("g0", "g1") else 0.235


def plan(nodes):
    m = len(nodes)
    succ = [[] for _ in range(m)]
    left = [len(x["deps"]) for x in nodes]
    for n, x in enumerate(nodes):
        for d in x["deps"]:
            succ[d].append(n)
    way = [0.0] * m
    for n in range(m - 1, -1, -1):
        way[n] = nodes[n]["cost"] + nodes[n]["lat"] + max([way[k] for k in succ[n]] + [0.0])
    start = [0.0] * m
    free, can, order = {}, {}, []
    for n in range(m):
        if not left[n]:
            can.setdefault(nodes[n]["q"], []).append(n)
    while len(order) < m:
        best = None
        for q in can:
            if can[q]:
                t = max(free.get(q, 0.0), min(start[n] for n in can[q]))
                if best is None or t < best[0]:
                    best = (t, q)
        t, q = best
        now = [n for n in can[q] if start[n] <= t + 1e-9]
        n = max(now, key=lambda k: (way[k], -k))
        for k in sorted(can[q], key=lambda k: -way[k]):
            if way[k] > way[n] + GAP and start[k] < t + PATIENCE * nodes[n]["cost"]:
                n = k
                break
        t = max(t, start[n])
        can[q].remove(n)
        order.append((t, len(order), n))
        free[q] = t + nodes[n]["cost"]
        for k in succ[n]:
            left[k] -= 1
            start[k] = max(start[k], t + nodes[n]["cost"] + nodes[n]["lat"])
            if not left[k]:
                can.setdefault(nodes[k]["q"], []).append(k)
    return [n for _, _, n in sorted(order)]


def relay(g, core, T, topo):
    sent = 0
    for t in range(RO - 1):
        d = 1 + t % (N - 1)
        for r in range(N):
            a, b = T.cores[r], T.cores[(r + d) % N]
            if a not in topo.cores_of(core):
                continue
            rel = routes(topo, a, b)
            if core not in rel:
                continue
            k, w = rel.index(core), 272 // len(rel)
            g.wait_ge(T.sem["in%d" % t], HOP)
            rid, pid = topo.addr(b, core)
            g.remote_dma(T["F%d" % (t + 1)][:, 256 + k * w:256 + (k + 1) * w], T["RB%d" % t][:, 0:w], T.sem["arr%d" % t], T.sem.sent,
                         pid, rid, topo.mask(core, b))
            sent += len(topo.engines(core, b))
    if sent:
        g.wait_ge(T.sem.sent, sent)


def rank_program(g, core, T, topo):
    rank = T.rank_of(core)
    if rank is None:
        return relay(g, core, T, topo)
    ENG = {"v": g.vector, "s": g.scalar, "pe": g.tensor, "gq": g, "sync": g.sync}
    V = g.vector
    nodes, lastw, readers = [], {}, {}

    def add(q, emit, reads, writes, cost, lat, sem, inc):
        reads, writes = reads.split(), writes.split()
        deps = set(lastw[k] for k in reads + writes if k in lastw)
        for k in writes:
            deps |= readers.get(k, set())
        n = len(nodes)
        nodes.append({"q": q, "emit": emit, "deps": deps, "cost": cost, "lat": lat, "sem": sem, "inc": inc})
        for k in writes:
            lastw[k] = n
            readers[k] = set()
        for k in reads:
            readers.setdefault(k, set()).add(n)

    def run(q, fn, reads, writes, *a, **kw):
        add(q, lambda: fn(*a, **kw), reads, writes, guess(q, writes.split()[0]), LAT, q, 1)

    def load(q, out, in_, sem, key, reads=""):
        add(q, lambda: ENG[q].dma_start(out, in_), reads, key, 0.06, 1.9, sem, 16)

    def issue():
        cnt, seen, tok = {}, {}, {}
        for n in plan(nodes):
            x = nodes[n]
            q = x["q"]
            need = {}
            for d in x["deps"]:
                if d in tok and not (q == "pe" and tok[d][0] == "pe"):
                    need[tok[d][0]] = max(need.get(tok[d][0], 0), tok[d][1])
            for sm in sorted(need):
                if q in ENG and seen.get((q, sm), 0) < need[sm]:
                    ENG[q].wait_ge(T.sem[sm], need[sm])
                    seen[(q, sm)] = need[sm]
            ins = x["emit"]()
            if x["sem"]:
                cnt[x["sem"]] = cnt.get(x["sem"], 0) + x["inc"]
                tok[n] = (x["sem"], cnt[x["sem"]])
                if ins is not None:
                    ins.then_inc(T.sem[x["sem"]], x["inc"])
        return cnt, seen

    def tt(reads, w, out, a, b, op):
        run("v", V.tensor_tensor, reads, w, out, a, b, op)

    def ts(reads, w, out, a, s1, op0, s2=None, op1=None):
        if op1 is None:
            run("v", V.tensor_scalar, reads, w, out, a, s1, None, op0)
        else:
            run("v", V.tensor_scalar, reads, w, out, a, s1, s2, op0, op1)

    def cp(reads, w, out, a):
        run("v", V.tensor_copy, reads, w, out, a)

    def scan(reads, w, out, d0, d1, op):
        run("v", V.tensor_tensor_scan, reads, w, out, d0, d1, 0.0, OP.mult, op)

    def act(reads, w, out, a, func=AF.Copy, **kw):
        run("s", g.scalar.activation, reads, w, out, a, func, **kw)

    def mms(reads, w, calls):
        def emit():
            for c in calls:
                ins = g.tensor.matmul(*c)
            return ins
        add("pe", emit, reads, w, 0.9 if len(calls) == 16 else 1.7 if len(calls) == 4 else 0.25 * len(calls), LAT, "pe", 1)

    def lf(j, n=1):
        return T.LF[:, 16 * j:16 * j + 16 * n]

    def li(j, n=1):
        return T.LI[:, 16 * j:16 * j + 16 * n]

    SG, SCL = T.SAV[:, 0:16], T.SAV[:, 16:32]
    ONES = T.ONEB[0:1, 0:128]

    load("sync", T.TT[:, 0:16], T.gs[:], "l_gs0", "tt0")
    load("sync", T.TT[:, 16:32], T.gs[:], "l_gs1", "tt1")
    load("sync", T.SKI[:], T.sk[:], "l_sk", "ski")
    load("sync", T.GFR[:], T.gf[:], "l_gfr", "gfr")
    load("sync", T.XR[:, 592:4096], T.x[:, 0:3504], "l_x0", "xr0")
    load("s", T.TT[:, 32:48], T.gf[:], "l_gf0", "tt2")
    load("s", T.TT[:, 48:64], T.gf[:], "l_gf1", "tt3")
    load("s", T.FRI[:], T.fr[:], "l_fr", "fri")
    load("s", T.TT[:, 64:80], T.gcl[:], "l_gc0", "tt4")
    load("s", T.TT[:, 80:96], T.gcl[:], "l_gc1", "tt5")
    load("s", T.XR[:, 0:592], T.x[:, 3504:4096], "l_x1", "xr1")
    load("s", T.THI[:], T.th[:], "l_th", "thi")
    XRK = "xr0 xr1 "

    run("v", V.memset, "", "oneb", T.ONEB[:], 1.0)
    run("v", V.memset, "", "onef", T.ONEF[:], 1.0)
    run("v", V.memset, "", "oneg", T.ONEG[:], 1.0)

    def sel(o, i, p, base, r, w):
        run("gq", g.affine_select, r, w, o, i, p, OP.is_equal, 0.0, base, 1)

    def iota(o, p, base, cm, w):
        run("gq", g.iota, "", w, o, p, base, cm, allow_small_or_imprecise_dtypes=True)
    iota(T.C16[:], [[16, 16]], KE, 0, "c16")
    iota(T.PIO[:], [[0, 16]], 0, 1, "pio")
    sel(T.R8[:], T.ONEB[0:8, 0:128], [[-1, 8], [0, 16]], 0, "oneb", "r8")
    sel(T.R16[:], T.ONEB[0:16, :], [[0, 16], [-1, 16]], 0, "oneb", "r16")
    iota(T.IOT[:], [[1, 256]], 0, 0, "iot")
    iota(T.KB[:], [[0, 16], [-1, 16]], 15, 0, "kb")
    sel(T.IDF[:], T.ONEG[:], [[-1, 128]], 0, "oneg", "idf")
    iota(T.BIA[:], [[1, 256]], 256, 0, "bia")
    ts("pio", "pm", T.PM[:], T.PIO[:], 15, OP.bitwise_and)
    ts("pio", "mui", T.MUI[:], T.PIO[:], 4, OP.arith_shift_right, 1, OP.bitwise_and)
    ts("c16", "bc15", T.BC15[:], T.C16[:], float(15 - KE), OP.add)
    cp("mui", "mu1", T.MU1[:], T.MUI[:])
    ts("mui", "mu0", T.MU0[:], T.MUI[:], -1.0, OP.mult, 1.0, OP.add)
    tt("pm c16", "lik", T.LIK[:], T.PM[:], T.C16[:], OP.add)
    ts("c16", "bcc", T.BCC[:], T.C16[:], float(-KE), OP.add, 0.0625, OP.mult)
    mms("r8", "p4", [(T.P4[:, 0:128], T.R8[:], T.R8[:], True, True)])
    mms("r16", "p0", [(T.P0[:, 0], T.R16[:, 0:128], T.R16[:], True, True)])
    for j in range(8):
        act("oneb", "sq", T.SQ[:, 256 * j:256 * j + 256], T.ONEB[:], scale=0.0)
    for j in range(2):
        act("oneb", "swp", T.SWP[:, 2 * j:2 * j + 2], T.ONEB[:], scale=0.0)
    for u in range(2):
        for gl in range(2):
            sel(T.SWP[:, 2 * u + gl, :, gl, :], T.ONEF[:, :, 0, :], [[-32, 4], [-1, 16]], -16 * u, "onef swp", "sw%d" % (2 * u + gl))

    run("v", V.transpose, "tt0 tt1 tt2 tt3 tt4 tt5", "tx", T.TX[:], T.TT[:])
    ts("tx mu0", "ta", T.TA[:], T.TX[:, :, 0, :], T.MU0[:, 0:1], OP.mult)
    ts("tx mu1", "tb", T.TB[:], T.TX[:, :, 1, :], T.MU1[:, 0:1], OP.mult)
    ts("fri", "frq", T.FRQ[:], T.FRI[:], 511, OP.bitwise_and)
    tt("ta tb", "tl", T.TL[:], T.TA[:], T.TB[:], OP.add)
    cp("gfr", "gfb", T.GFB[:], T.GFR[:])
    mms("r8 gfb", "p2", [(T.P2[:, 0:256], T.R8[:], T.GFB[:], True, True)])
    act("p2", "bg", T.BG[:], T.P2[:, 0:256])
    ts("fri", "m1", T.P6[:, 0:256], T.FRI[:], 2.0, OP.mult, float(KE), OP.add)
    ts("fri", "eq", T.P5[:, 0:256], T.FRI[:], 0.0, OP.is_lt, NEG, OP.mult)
    tt("m1 frq", "ow", T.OW[:], T.P6[:, 0:256], T.FRQ[:], OP.subtract)
    cp("tl", "sl", T.SL[:], T.TL[:, 0, :])
    tt("eq ow", "f0o", T.F0[:, 0:256], T.P5[:, 0:256], T.OW[:], OP.add)
    cp("tl", "fl", T.FL[:], T.TL[:, 1, :])
    act("f0o", "f0g", T.F0[:, 256:512], T.F0[:, 0:256])
    run("gq", g.affine_select, "ski", "skf", T.SKU[:], T.SKI[:], [[1, 1024]], OP.is_ge, 0.0, 0, 0)
    BANK = {"P5": "eq t2", "P6": "m1 m2"}
    for j, p in ((0, "P5"), (1, "P6")):
        cs = slice(512 * j, 512 * j + 512)
        ts("ski", BANK[p], T[p][:], T.SKI[:, cs], 1024.0, OP.is_ge, float(-(1 << 20) - 2 * B), OP.mult)
        act("skf", "sku%d" % j, T.SKU[:, cs], T.SKU[:, cs], AF.Identity, bias=float(KE + B), scale=1024.0)
    for j, p in ((0, "P5"), (1, "P6")):
        cs = slice(512 * j, 512 * j + 512)
        tt("%s sku%d" % (BANK[p], j), "skv", T.SKV[:, cs], T[p][:], T.SKU[:, cs], OP.add)
    cp("tl", "cl", T.CL[:], T.TL[:, 2, :])
    act("p0", "diag", T.DIAG[:], T.P0[:, 0])
    act("p4", "blkf", T.BLKF[:], T.P4[:, 0:128])
    act("p0", "dif", T.DIF[:], T.P0[:, 0, 0, :], scale=-2.0 * NEG)
    for q in range(16):
        act("p4", "sq", T.SQ[:, 128 * q + q:128 * q + 128:16], T.P4[:, q:128:16], scale=16.0)
    act("idf", "idb", T.IDB[:], T.IDF[:], scale=-NEG)
    act("f0o", "base", T.BASE[:], T.F0[:, 0:256])

    def later_constants():
        cp("thi", "thf", T.THF[:], T.THI[:])
        ts("diag thf", "thd", T.THD[:], T.DIAG[:], T.THF[:, 0:1], OP.mult)
        mms("blkf thd", "p2", [(T.P2[:, 0:256], T.BLKF[:], T.THD[:], True, True)])
        act("kb", "rst0", T.RST[:, 0:256], T.KB[:], AF.Sign, scale=-1.0, bias=15.0)
        act("kb", "rst1", T.RST[:, 256:512], T.KB[:], AF.Sign, scale=-1.0, bias=15.0)
        run("v", V.memset, "", "thr", lf(3), 8.0)
        act("oneb", "mk", T.MK[:], T.ONEB[:], AF.Identity, scale=0.0, bias=NEG)
        ts("tl", "l2", lf(2), T.TL[:, 0, :], 1024.0, OP.mult, float(KE), OP.add)
        run("v", V.memset, "", "npr", T.NPR[:, 0:256], NEG)
        run("v", V.memset, "", "npr", T.NPR[:, 256:512], -NEG)
        cp("tl", "sav", SCL, T.TL[:, 2, :])
        tt("tl l2", "sav", SG, T.TL[:, 1, :], lf(2), OP.add)
        ts("p2", "thw", T.THW[:], T.P2[:, 0:256], -1.0, OP.add)
        ts("p2", "tha", T.THA[:], T.P2[:, 0:256], 16.0, OP.mult, 15.0, OP.add)
        ts("thw", "thw", T.THW[:], T.THW[:], 1, OP.arith_shift_right)
        ts("thw", "thb", T.THB[:], T.THW[:], 16.0, OP.mult, 15.0, OP.add)
        cp("blkf", "blkh", T.BLKH[:], T.BLKF[:])
        cp("oneb", "oneh", T.ONEH[:], T.ONEB[0:1, 0:128])
        ts("iot", "nih", T.NIH[:], T.IOT[0:1, :], -1.0, OP.mult)
        new_saved_clause()

    def new_saved_clause():
        ts("sav", "i1", li(1), SG, 10, OP.arith_shift_right, 2047, OP.bitwise_and)
        ts("i1", "l5", lf(5), li(1), -560.0, OP.add)
        tt("l5 sav", "l6", lf(6), lf(5), SCL, OP.mult)
        ts("l6", "i2", li(2), lf(6), 32.0, OP.add)
        ts("i2", "i5", li(5), li(2), 5, OP.arith_shift_right, 1023, OP.bitwise_and)
        ts("i5", "l7", lf(7), li(5), 1024.0, OP.mult)
        tt("l7 lik", "l4", lf(4), lf(7), T.LIK[:], OP.add)

    def recs(o, n, key):
        c = slice(o, o + n)
        ts("xi" + key, "pi" + key, T.PI[:, c], T.XI[:, c], 10, OP.arith_shift_right, 2047, OP.bitwise_and)
        ts("xi" + key, "qi" + key, T.QI[:, c], T.XI[:, c], 1023, OP.bitwise_and)
        tt("pi%s qi%s" % (key, key), "zi" + key, T.ZI[:, c], T.PI[:, c], T.QI[:, c], OP.mult)
        ts("zi" + key, "ri" + key, T.RI[:, c], T.ZI[:, c], 4, OP.arith_shift_right, 4095, OP.bitwise_and)
        cp("ri" + key, "rl" + key, T.RL[:, c], T.RI[:, c])

    def save_numbers(parity):
        tt("l18 l10", "l22", lf(19), lf(18), lf(10), OP.add)
        tt("i6 i7 sav", "l20", lf(20, 2), li(6, 2), T.SAV[:], OP.subtract)
        if parity:
            cp("p2", "i12", li(12), T.P2[:, 256:272])
        tt("l20 l18 l22", "l21", lf(22, 2), lf(20, 2), lf(18, 2), OP.mult)
        if parity:
            ts("i12", "i13", li(13), li(12), 1, OP.bitwise_and)
        tt("l21 sav", "sav", T.SAV[:], lf(22, 2), T.SAV[:], OP.add)
        if parity:
            ts("i13", "thr", lf(3), li(13), -1.0, OP.mult, 8.0, OP.add)

    def swap(p, j, stop):
        mms("xt sw0 sw1 sw2 sw3", p.lower(), [(T[p][:, 0, :, u, :], T.SWP[:, 2 * u + gl], T.XT[:, 8 * j:8 * j + 8, gl, :],
                                               u + gl == 0, stop and u + gl == 2) for u in range(2) for gl in range(2)])

    def sv_payload():
        tt("p0 thb", "sv", T.SV[:], D, T.THB[:], OP.is_le)
        mms("sv idb", "p7", [(T.P7[:, 0], T.IDB[:], T.SV[:], False, True)])

    sent = 0
    D = T.P0[:, 0]
    EQ, T2 = T.P5[:, 0:256], T.P5[:, 256:512]
    M1, M2 = T.P6[:, 0:256], T.P6[:, 256:512]
    for t in range(RO):
        F = T["F%d" % t]
        fo, fg, fs = "f%do" % t, "f%dg" % t, "f%ds" % t
        last = t == RO - 1
        if t == 0:
            tt("skv sl bg", "cg", T.CG[:], T.SKV[:].indirect(T.SL[:]), T.BG[:], OP.add)
        else:
            act(fg, "p3", T.P3[:, 0], F[:, 256:512])
            act("hl " + fo + " " + fg, "wc", T.WC[:], F[:, 0:512].indirect(T.HL[:]))
            cp(fs, "sl", T.SL[:], F[:, 512:528])
            tt("skv sl bia", "cg", T.CG[:], T.SKV[:].indirect(T.SL[:]), T.BIA[:], OP.add)
        for k in range(2):
            c = slice(128 * k, 128 * k + 128)
            if t == 0:
                tt(fo + " " + fg + " fl cg", "xig%d" % k, T.XI[:, c], F[:, 0:512].indirect(T.FL[:, 8 * k:8 * k + 8]), T.CG[:, c], OP.max)
            else:
                tt("cg p3", "xig%d" % k, T.XI[:, c], T.P3[:, 0, 8 * k:8 * k + 8, :], T.CG[:, c], OP.max)
            recs(128 * k, 128, "g%d" % k)
        for j, (a, b) in enumerate(PARTS):
            if j not in HELP[t]:
                act(XRK + "rlg%d" % (a // 8), "u%d" % j, T.U[:, 256 * a:256 * b], T.XR[:].indirect(T.RL[:, 16 * a:16 * b]))
        if t == 0:
            for q in range(16):
                act("p4 dif", "tq", T.TQ[:, 128 * q:128 * q + 128], T.P4[:, 0:128], scale=T.DIF[:, q:q + 1])
            tt("skv cl iot", "vc", T.VC[:], T.SKV[:].indirect(T.CL[:]), T.IOT[:], OP.add)
            tt("vc " + fo, "xc", T.XC[:], T.VC[:], F[:, 0:256], OP.max)
            ts(fo, "eq", EQ, F[:, 0:256], -2.0, OP.mult, NEG, OP.add)
        else:
            tt("m2 wc", "xc", T.XC[:], M2, T.WC[:], OP.max)
        ts("xig0 xig1", "mg", T.MG[:], T.XI[:, 0:256], B - 1, OP.bitwise_and)
        tt("eq mg", "t2", T2, EQ, T.MG[:], OP.min)
        tt("t2 xc", "xic", T.XI[:, 256:512], T2, T.XC[:], OP.max)
        run("gq", g.affine_select, "xig0 xig1 xic", "xf", T.XF[:], T.XI[:], [[1, 512]], OP.is_ge, 0.0, 0, 0)
        recs(256, 256, "c")
        if t == 0:
            later_constants()
        mms("oneb kb", "p0", [(D, ONES, T.KB[0:1, :], True, False)])
        for j, (a, b) in enumerate(PARTS):
            if j in HELP[t]:
                cp(XRK + "rlg1 db1", "u%d" % j, T.U[:, 256 * a:256 * b], T.XR[:].indirect(T.RL[:, 16 * a:16 * b]))
            tt(XRK + "rlc u%d" % j, "db%d" % j, T.DB[:, 256 * a:256 * b], T.XR[:].indirect(T.RL[:, 256 + 16 * a:256 + 16 * b]),
               T.U[:, 256 * a:256 * b], OP.subtract)
            act("db%d" % j, "ab%d" % j, T.AB[:, a:b], T.DB[:, 256 * a:256 * b], AF.Abs)
        for j, (a, b, need) in enumerate(SUMS):
            mms(need + " sq", "p0", [(T.P0[:, 0, a:b, :], T.SQ[:, 128 * q:128 * q + 128], T.AB[:, a:b, q, :], False, j == len(SUMS) - 1 and q == 15)
                                     for q in range(16)])
        mms("oneb npr", "p2", [(T.P2[:, 0:256], ONES, T.NPR[0:1, 0:256], True, False)])
        act("xf", "flg", T.FLG[:], T.XF[:, 256:512], AF.Relu, bias=float(-16 * (B - 1)), scale=16.0)
        run("v", V.transpose, "xf", "xt", T.XT[:], T.XF[:])
        swap("P1", 0, True)
        if t:
            new_saved_clause()
        tt("t2 flg", "eq", EQ, T2, T.FLG[:], OP.subtract)
        tt("eq mk", "ya", T.YA[:], EQ, T.MK[:], OP.max)
        tt("p0 tha", "nov", T.NOV[:], D, T.THA[:], OP.is_le)
        scan("rst0 nov", "ns", T.NS[:], T.RST[:, 0:256], T.NOV[:], OP.add)
        tt("p0 nov", "ky", T.KY[:], D, T.NOV[:], OP.mult)
        tt("ns thr", "l8", T.SB[:], T.NS[:, 15::16], lf(3), OP.is_gt)
        mms("l8 tq", "p2", [(T.P2[:, q:256:16], T.TQ[:, 128 * q:128 * q + 128], T.SB[:], False, q == 15) for q in range(16)])
        swap("P7", 1, False)
        mms("oneb npr", "p3", [(T.P3[:], ONES, T.NPR[0:1, :], True, False)])
        scan("rst0 ky", "km", T.KM[:], T.RST[:, 0:256], T.KY[:], OP.max)
        tt("ns thr", "l10", lf(10), T.NS[:, 15::16], lf(3), OP.is_le)
        tt("km bc15 ky", "mask", T.MASK[:], T.KM[:].indirect(T.BC15[:]), T.KY[:], OP.is_equal)
        tt("l10 sav", "l11", lf(11), lf(10), SG, OP.mult)
        tt("p1 mask", "mx0", T.MX[:, 0:256], T.P1[:, 0], T.MASK[:], OP.mult)
        scan("rst0 mx0", "sc0", T.SC[:, 0:256], T.RST[:, 0:256], T.MX[:, 0:256], OP.add)
        if last:
            sv_payload()
        tt("sc0 l8", "l12", lf(12), T.SC[:, 15:256:16], T.SB[:], OP.mult)
        tt("p2 ya", "m1", M1, T.P2[:, 0:256], T.YA[:], OP.min)
        tt("l12 l11", "i6", li(6), lf(12), lf(11), OP.add)
        tt("m1 base", fo, F[:, 0:256], M1, T.BASE[:], OP.max)
        if not last:
            ts("i6", "i8", li(8), li(6), 1023, OP.bitwise_and)
            ts("i6", "i9", li(9), li(6), 10, OP.arith_shift_right, 2047, OP.bitwise_and)
            ts("i8", "fl", T.FL[:], li(8), -16.0, OP.add)
            C = T["COL%d" % t]
            ts("i9", "cols", C[:, 256:272], li(9), -592.0, OP.add)
            cp("fl " + fo + " " + fg, "col", C[:, 0:256], F[:, 0:512].indirect(T.FL[:]))
            d = 1 + t % (N - 1)
            dst = T.cores[(rank + d) % N]
            rel = routes(topo, core, dst)
            tr = []
            if rel:
                w = 272 // len(rel)
                for k, c in enumerate(rel):
                    rid, pid = topo.addr(c, core)
                    es = topo.engines(core, c)
                    tr.append(RemoteDMATransfer(dst_ids=[DstId(rid=rid, pnc=pid)], dma_engine_mask=only(es[HOP * k:], HOP),
                                                remote_sem=T.sem["in%d" % t], src=C[:, k * w:(k + 1) * w], dst=T["RB%d" % t][:, 0:w]))
                add("gq", lambda tr=tr: hand(g.remote_dma_fused(tr, local_sem=T.sem.sent)), "cols col", "go", 1.0, 5.0, None, 0)
                sent += HOP * len(rel)
            else:
                rid, pid = topo.addr(dst, core)
                add("gq", lambda a=(T["F%d" % (t + 1)][:, 256:528], C[:], T.sem["arr%d" % t], T.sem.sent, pid, rid, topo.mask(core, dst)):
                    hand(g.remote_dma(*a)), "cols col", "go", 1.0, 3.0, None, 0)
                sent += len(topo.engines(core, dst))
            src = T.cores[(rank - d) % N]
            rin = routes(topo, src, core)
            n = sum(len(topo.engines(c, core)) for c in rin) if rin else len(topo.engines(src, core))
            add("net", lambda: None, "go", "f%dg f%ds" % (t + 1, t + 1), 0.0, 0.0, "arr%d" % t, n)
            act(fo, "f%do" % (t + 1), T["F%d" % (t + 1)][:, 0:256], F[:, 0:256])
            act(fo, "wn", T.WN[:], F[:, 0:256], scale=-1.0)
            act("m1 m2 " + fo, "ya", T.YA[:], M1)
            mms("l8 diag", "p2", [(T.P2[:, 256:272], T.DIAG[:, 0:128], T.SB[:], True, True)])
            sv_payload()
        tt("l10 l4", "l13", lf(13), lf(10), lf(4), OP.mult)
        tt("p7 mask", "mx1", T.MX[:, 256:512], T.P7[:, 0], T.MASK[:], OP.mult)
        scan("rst1 mx1", "sc1", T.SC[:, 256:512], T.RST[:, 256:512], T.MX[:, 256:512], OP.add)
        tt("sc1 l8", "l14", lf(14), T.SC[:, 271::16], T.SB[:], OP.mult)
        ts("sc1", "l17", lf(17), T.SC[:, 271::16], float(2 * B), OP.is_ge)
        tt("l13 l14", "i10", li(10), lf(13), lf(14), OP.add)
        tt("l17 l8", "l18", lf(18), lf(17), T.SB[:], OP.mult)
        ts("i10", "i14", li(14), li(10), 1023, OP.bitwise_and)
        ts("i10", "i11", li(11), li(10), 10, OP.arith_shift_right, 2047, OP.bitwise_and)
        act("l18", "s2a", T.S2[:, 0, :], lf(18))
        act("l18", "s2b", T.S2[:, 1, :], lf(18), scale=-1.0)
        mms("s2a s2b tq", "p3", [(T.P3[:, :, :, q], T.TQ[:, 128 * q:128 * q + 128], T.S2[:], False, q == 15) for q in range(16)])
        if not last:
            ts("i14", "l16", lf(16), li(14), -16.0, OP.add)
        ts("i11", "i7", li(7), li(11), -592.0, OP.add)
        if not last:
            tt("l16 bcc diag", "eh", T.EH[:], lf(16).indirect(T.BCC[:]), T.DIAG[:], OP.mult)
            cp("i7", "cl", T.CL[:], li(7))
            act("skv cl", "vc", T.VC[:], T.SKV[:].indirect(T.CL[:]))
            mms("eh blkh oneh nih", "p4", [(T.P4[:, 0:256], T.BLKH[:], T.EH[:], True, True), (T.P4[:, 256:512], T.ONEH[:], T.NIH[:], True, False),
                                           (T.P4[:, 256:512], T.BLKH[:], T.EH[:], False, True)])
            cp("l16", "hl", T.HL[:], lf(16))
            act("p4", "ha", T.HA[:], T.P4[:, 256:512], AF.Abs)
            tt("p3 ya", "m2", M2, T.P3[:, 0], T.YA[:], OP.min)
            tt("p3 ya", "mk", T.MK[:], T.P3[:, 1], T.YA[:], OP.min)
            tt("m2 base", "base", T.BASE[:], M2, T.BASE[:], OP.max)
            act("ha", "p3", T.P3[:, 1], T.HA[:], AF.Identity, bias=-NEG, scale=2.0 * NEG)
            tt("p4 vc ha", "m2", M2, T.P4[:, 0:256], T.VC[:], OP.add)
            save_numbers(True)
            tt("p3 wn", "eq", EQ, T.P3[:, 1], T.WN[:], OP.min)
        else:
            save_numbers(False)
    act("m1 m2 f3o", "ya", T.YA[:], M1)
    cp("f3o", "pig0 pig1", T.PI[:, 0:256], T.F3[:, 0:256])
    ts("pig0 pig1", "qig0 qig1", T.QI[:, 0:256], T.PI[:, 0:256], 1023, OP.bitwise_and)
    ts("f3o ya", "m2", M2, T.F3[:, 0:256], -606240.0, OP.add)
    tt("m2 qig0 qig1 ya", "yo", T.YO[:], M2, T.QI[:, 0:256], OP.add)
    tt("p3 ya", "m2", M2, T.P3[:, 1], T.YA[:], OP.min)
    ts("yo", "ym", T.YM[:], T.YO[:], -1.0, OP.max)
    ts("m2", "p2", T.P2[:, 0:256], M2, 0.0, OP.is_ge)
    tt("p2 ym", "yo", T.YO[:], T.P2[:, 0:256], T.YM[:], OP.add)
    load("sync", T.yf[:], T.YO[:], "out", "yf", "yo")

    srcs = [("i6", li(6)), ("i10", li(10)), ("sav", SG)]
    for j, (key, src) in enumerate(srcs):
        ts(key, "pic", T.PI[:, 256 + 16 * j:272 + 16 * j], src, 10, OP.arith_shift_right, 2047, OP.bitwise_and)
        ts(key, "qic", T.QI[:, 256 + 16 * j:272 + 16 * j], src, 1023, OP.bitwise_and)
    ts("pic", "mx0", T.MX[:, 0:48], T.PI[:, 256:304], 512.0, OP.mult, float(-592 * 512 - 16), OP.add)
    for k in range(2):
        tt("mx0 qic", "fld%d" % k, T.FLD[:, 0:3, k, :], T.MX[:, 0:48], T.QI[:, 256:304], OP.add)
        cp("sav", "fle%d" % k, T.FLD[:, 3, k, :], SCL)
    run("v", V.transpose, "fld0 fld1 fle0 fle1", "flt", T.FLT[:], T.FLD[:])
    ts("flt mu0", "fo", T.FO[:], T.FLT[:, :, 0, :], T.MU0[:, 0:1], OP.mult)
    ts("flt mu1", "fp", T.FP[:], T.FLT[:, :, 1, :], T.MU1[:, 0:1], OP.mult)
    tt("fo fp", "fo", T.FO[:], T.FO[:], T.FP[:], OP.add)
    for j, y in enumerate((T.yg, T.yc, T.ysg, T.yk)):
        load("sync" if j % 2 else "s", y[:], T.FO[:, j, :], "out", "y%d" % j, "fo")
    cnt, seen = issue()
    g.sync.wait_ge(T.sem.out, cnt["out"])
    g.wait_ge(T.sem.sent, sent)
    for q in ("v", "s", "pe", "gq"):
        g.sync.wait_ge(T.sem[q], cnt[q])
    for sm in LOADS:
        if not any(k[1] == sm for k in seen):
            g.sync.wait_ge(T.sem[sm], 16)
